import numpy as np
import ml_dtypes


def mxq(x, axis, fmt="e4m3"):
    dtype, down = {"e4m3": (ml_dtypes.float8_e4m3fn, 7), "e5m2": (ml_dtypes.float8_e5m2, 14)}[fmt]
    v = np.moveaxis(np.asarray(x, np.float32).astype(ml_dtypes.bfloat16).astype(np.float64), axis, -1)
    blocks = v.reshape(v.shape[:-1] + (-1, 32))
    amax = np.abs(blocks).max(-1, keepdims=True)
    byte = np.maximum(np.where(amax > 0, np.frexp(amax)[1] - 1 + 127, 0) - down, 1)
    scale = np.exp2(byte - 127.0)
    codes = (blocks / scale).astype(np.float32).astype(dtype).astype(np.float64)
    return np.moveaxis((codes * scale).reshape(v.shape), -1, axis)


WIDE = False


def mx_kscale(k):
    if not WIDE:
        return np.ones(k)
    levels = np.array([10, -10, 5, -5, 0])
    if k % 512:
        return np.exp2(np.random.permutation(np.resize(levels, k // 32))).repeat(32)
    a = np.empty((k // 512, 16))
    for p in range(k // 512):
        a[p, :8] = np.random.permutation(np.resize(levels, 8))
        for g in range(8):
            far = levels[np.abs(levels - a[p, g]) >= 10]
            a[p, g + 8] = far[np.random.randint(len(far))]
    return np.exp2(a.ravel()).repeat(32)


BF16 = ml_dtypes.bfloat16


def bf(x):
    return np.asarray(x, np.float32).astype(BF16)


def f64(x):
    return np.asarray(x).astype(np.float64)


E2M1 = np.array([0.0, 0.5, 1.0, 1.5, 2.0, 3.0, 4.0, 6.0, -0.0, -0.5, -1.0, -1.5, -2.0, -3.0, -4.0, -6.0])


def pack_weight(w, fmt):
    k, n = w.shape
    w = f64(bf(w)).reshape(k // 32, 32, n)
    amax = np.abs(w).max(1)
    if fmt == "e4m3":
        byte = np.frexp(amax)[1] - 1 + 127 - 7
    else:
        mant, ex = np.frexp(amax / 6.0)
        byte = np.where(mant > 0.5, ex, ex - 1) + 127
    byte = np.clip(np.where(amax > 0, byte, 1), 1, 254)
    scaled = (w * np.exp2(127.0 - byte)[:, None, :]).reshape(k, n).astype(np.float32)
    by_word = np.ascontiguousarray(scaled.reshape(k // 512, 128, 4, n).transpose(0, 1, 3, 2))
    if fmt == "e4m3":
        words = by_word.astype(ml_dtypes.float8_e4m3fn).view(np.uint8)
    else:
        c = by_word.astype(ml_dtypes.float4_e2m1fn).view(np.uint8) & 0xF
        words = c[..., 0::2] | (c[..., 1::2] << 4)
    return np.ascontiguousarray(words), np.ascontiguousarray(byte.astype(np.uint8).reshape(k // 512, 16, n))


def unpack_weight(words, scales, fmt):
    g, p, n, _ = words.shape
    if fmt == "e4m3":
        vals = np.ascontiguousarray(words).view(ml_dtypes.float8_e4m3fn).astype(np.float64)
    else:
        nib = np.empty((g, p, n, 4), np.uint8)
        nib[..., 0::2] = words & 0xF
        nib[..., 1::2] = words >> 4
        vals = E2M1[nib]
    vals = vals * np.repeat(np.exp2(scales.astype(np.float64) - 127.0), 8, axis=1)[..., None]
    return vals.transpose(0, 1, 3, 2).reshape(g * 512, n)
def pack4(w):
    words, scales = pack_weight(w, "e2m1")
    return words.reshape(words.shape[0], 128, -1), scales


def unpack4(words, scales):
    return unpack_weight(words.reshape(words.shape[0], 128, -1, 2), scales, "e2m1")


def planes(Y):
    n, m = Y.shape
    b = f64(bf(Y)).reshape(n // 32, 32, m)
    amax = np.abs(b).max(1)
    byte = np.clip(np.where(amax > 0, np.frexp(amax)[1] - 1 + 127 - 7, 1), 1, 254)
    codes = (b * np.exp2(127.0 - byte)[:, None, :]).reshape(n, m).astype(np.float32).astype(ml_dtypes.float8_e4m3fn).view(np.uint8)
    words = codes.reshape(n // 512, 128, 4, m).transpose(0, 1, 3, 2)
    return np.ascontiguousarray(words), np.ascontiguousarray(byte.astype(np.uint8).reshape(n // 512, 16, m))


B, K, T, J = 2048, 1024, 1024, 512


def setup_inputs():
    randn = np.random.randn
    f_cov, f_day, f_int = mx_kscale(K), mx_kscale(T), mx_kscale(T)
    x = randn(B, K)
    x[:, 0] = 1.0
    x_words, x_scales = pack_weight(np.ascontiguousarray((x * f_cov).T), "e4m3")
    w = 0.7 * (randn(K, 1) + randn(K, T)) / np.sqrt(K)
    w[0] = 0.3 * randn(T) - 1.0
    day = (np.arange(T) + 0.5) / T
    c = np.where(day[None, :] <= day[:, None], np.abs(1.0 + 0.25 * randn(T, T)), 0.1 * np.abs(randn(T, T)))
    cum_words, cum_scales = pack4(c * f_day[:, None] / f_int[None, :])
    hor = (np.arange(J) + 0.5) / J
    a = np.abs(randn(T, J)) * np.exp(-3.0 * np.abs(day[:, None] - hor[None, :])) / T
    return {"x_words": x_words, "x_scales": x_scales, "w": bf(w / f_cov[:, None]),
            "season": bf(0.3 * np.exp(0.3 * randn(T)) * f_int),
            "cum_words": cum_words, "cum_scales": cum_scales, "a": bf(a / f_day[:, None]),
            "lead": bf(0.05 * np.abs(randn(T)) / f_int),
            "pace": bf(0.03 * np.exp(0.3 * randn(B))), "value": bf(2.0 * np.exp(0.8 * randn(J)))}

def reference(x_words, x_scales, w, season, cum_words, cum_scales, a, lead, pace, value):
    x = unpack_weight(x_words, x_scales, "e4m3").T
    logits = x @ mxq(f64(w), 0, "e4m3")
    loss = np.log(1.0 + np.exp(logits)) * f64(season)[None, :]
    c = unpack4(cum_words, cum_scales)
    expo = (c.T @ mxq(f64(a), 0, "e4m3")) + f64(lead)[:, None]
    h = mxq(loss, 1, "e4m3") @ mxq(expo, 0, "e4m3")
    y = np.exp(-f64(pace)[:, None] * h) * f64(value)[None, :]
    Y = y.T
    words, scales = planes(Y)
    return y, words, scales

@@ -1,0 +1,486 @@
+from contextlib import ExitStack
+
+import concourse.mybir as mybir
+from concourse.masks import make_identity
+
+B, K, T, J = 2048, 1024, 1024, 512
+FLOPS = 2 * (B * K * T + T * T * J + B * T * J)
+
+F32 = mybir.dt.float32
+BF16 = mybir.dt.bfloat16
+I32 = mybir.dt.int32
+U32 = mybir.dt.uint32
+U8 = mybir.dt.uint8
+FP8X4 = mybir.dt.float8_e4m3fn_x4
+FP4X4 = mybir.dt.float4_e2m1fn_x4
+ACT = mybir.ActivationFunctionType
+ALU = mybir.AluOpType
+
+P = 128
+PACK = 4
+GROUP = P * PACK
+PASSES = K // GROUP
+DAY_GROUPS = T // GROUP
+TILES = B // P
+CHUNK = 2 * P
+BANK = 512
+SOFTPLUS_CAP = 8.0
+
+FIRST_TILES = 10
+LN_AHEAD = 7
+EARLY_TILES = 8
+EARLY_STEP = 5
+LN_STEP = 8
+LATE_STEP = 12
+VEC_BANKS = 3
+EXPO_FIRST = 8
+X_LOADS = ((0, 1), (1, 2), (2, 3), (3, 5), (5, 8))
+LAST_PAIR = TILES - 2
+
+
+def loss_ready(m):
+    return m + 1 if m >= LAST_PAIR else m // 2 * 2 + 2
+
+
+EXP_STEP = [
+    EARLY_STEP + m // 2 if m < EARLY_TILES else max(loss_ready(m), LATE_STEP + (m - EARLY_TILES) // 2)
+    for m in range(TILES)
+]
+WEIGH_STEP = [s + 1 for s in EXP_STEP]
+ROUND_STEP = WEIGH_STEP
+TURN_STEP = [max(LATE_STEP + 1 + c // 2, EXP_STEP[2 * c + 1] + 2) for c in range(TILES // 2)]
+QY_STEP = [s + 1 for s in TURN_STEP]
+TANH_MM = [i // 2 if i < 4 else i // 2 + 1 for i in range(12)]
+TANH_RD = [max(2, s) for s in TANH_MM]
+SPLIT = "VG" * (TILES - 1) + "VV"
+ROUND_ON = "G" * EARLY_TILES + "S" * (LAST_PAIR - EARLY_TILES) + "VV"
+
+
+def tile_churn_survival_horizons_k4_kernel(
+    tc, x_words, x_scales, w, season, cum_words, cum_scales, a, lead, pace, value, out_0, out_1, out_2
+):
+    nc = tc.nc
+    with ExitStack() as ctx:
+        keep = ctx.enter_context(tc.tile_pool(name="keep", bufs=1))
+        raw_pool = ctx.enter_context(tc.tile_pool(name="raw", bufs=4))
+        stage = ctx.enter_context(tc.tile_pool(name="stage", bufs=3))
+        tanh_pool = ctx.enter_context(tc.tile_pool(name="tanh", bufs=max(FIRST_TILES, TILES - FIRST_TILES)))
+        ln_pool = ctx.enter_context(tc.tile_pool(name="ln", bufs=LN_AHEAD + 1))
+        y_pool = ctx.enter_context(tc.tile_pool(name="y", bufs=5))
+        vec_banks = ctx.enter_context(tc.psum_pool(name="vec_banks", bufs=VEC_BANKS))
+        act_banks = ctx.enter_context(tc.psum_pool(name="act_banks", bufs=7 - VEC_BANKS))
+        const_banks = ctx.enter_context(tc.psum_pool(name="const_banks", bufs=1))
+        ctx.enter_context(tc.manual_schedule(engines={mybir.EngineType.Activation, mybir.EngineType.DVE, mybir.EngineType.SP}))
+
+        def load_rows(src, kp, cols):
+            raw = raw_pool.tile([P, PACK, GROUP], BF16, name="raw")
+            nc.sync.dma_start(
+                out=raw[:], in_=src[kp * GROUP : (kp + 1) * GROUP, cols].rearrange("(p j) n -> p j n", j=PACK)
+            )
+            return raw
+
+        def load_scale_rows(queue, plane, src):
+            for q in range(4):
+                queue.dma_start(
+                    out=plane[32 * q : 32 * q + 4, :, :].bitcast(I32),
+                    in_=src[:, 4 * q : 4 * q + 4, :].rearrange("g r n -> r g n").bitcast(I32),
+                )
+
+        x_codes = {}
+
+        def load_x(first, last):
+            words = keep.tile([P, PASSES, (last - first) * CHUNK], U32, name="x_codes_%d" % first, align_bytes=64)
+            src = x_words.rearrange("g p n t -> p g (n t)")[:, :, first * CHUNK * PACK : last * CHUNK * PACK]
+            nc.sync.dma_start(out=words[:].bitcast(I32), in_=src.bitcast(I32))
+            for c in range(first, last):
+                x_codes[c] = (words, (c - first) * CHUNK)
+
+        x_plane = keep.tile([P, PASSES, B], U8, align_bytes=64)
+        cum_plane_raw = keep.tile([P, PASSES, T], U8, align_bytes=64)
+        vec_rows = keep.tile([P, GROUP], BF16)
+        identity = keep.tile([P, P], F32)
+        nc.vector.memset(x_plane[:].rearrange("p g n -> p (g n)").bitcast(I32), 0)
+        nc.gpsimd.memset(cum_plane_raw[:].rearrange("p g n -> p (g n)").bitcast(I32), 0)
+        nc.gpsimd.memset(vec_rows[:], 0.0)
+        make_identity(nc, identity[:])
+        identity_bf16 = keep.tile([P, P], BF16)
+        make_identity(nc, identity_bf16[:])
+
+        w_raw = {}
+        w_raw[0, 0] = load_rows(w, 0, slice(0, GROUP))
+        w_raw[1, 0] = load_rows(w, 1, slice(0, GROUP))
+        load_scale_rows(nc.sync, x_plane, x_scales)
+        load_x(*X_LOADS[0])
+        load_x(*X_LOADS[1])
+        w_raw[0, 1] = load_rows(w, 0, slice(GROUP, 2 * GROUP))
+        load_x(*X_LOADS[2])
+        w_raw[1, 1] = load_rows(w, 1, slice(GROUP, 2 * GROUP))
+        load_x(*X_LOADS[3])
+        vec_raw = keep.tile([P, GROUP], BF16)
+        nc.sync.dma_start(out=vec_raw[0:2, :], in_=season.rearrange("(g n) -> g n", n=GROUP))
+        nc.sync.dma_start(out=vec_raw[2:4, :], in_=lead.rearrange("(g n) -> g n", n=GROUP))
+        nc.sync.dma_start(out=vec_raw[32:36, :], in_=pace.rearrange("(g n) -> g n", n=GROUP))
+        nc.sync.dma_start(out=vec_raw[64:65, :], in_=value.rearrange("(g n) -> g n", n=GROUP))
+
+        w_codes, w_planes, w_grouped = {}, {}, {}
+
+        def group_w(kp, g, t, on_scalar):
+            if (kp, g) not in w_grouped:
+                w_grouped[kp, g] = stage.tile([P, GROUP * PACK], BF16, name="grouped", align_bytes=64)
+            dst = w_grouped[kp, g][:, t * GROUP : (t + 1) * GROUP].rearrange("p (c i j) -> p c j i", i=4, j=PACK)
+            src = w_raw[kp, g][:].rearrange("p j (c t i) -> p t c j i", t=PACK, i=4)[:, t]
+            if on_scalar:
+                nc.scalar.activation(out=dst, in_=src, func=ACT.Copy, scale=-1.0)
+            else:
+                nc.vector.tensor_scalar(out=dst, in0=src, scalar1=-1.0, scalar2=None, op0=ALU.mult)
+
+        def quantize_w(kp, g, u):
+            if (kp, g) not in w_codes:
+                w_codes[kp, g] = keep.tile([P, GROUP], U32, name="w_codes_%d%d" % (kp, g), align_bytes=64)
+                w_planes[kp, g] = keep.tile([P, GROUP], U8, name="w_plane_%d%d" % (kp, g), align_bytes=64)
+            cols = slice(u * 2 * P, (u + 1) * 2 * P)
+            nc.vector.quantize_mx(
+                out=w_codes[kp, g][:, cols].bitcast(FP8X4),
+                scales=w_planes[kp, g][:, cols],
+                in_=w_grouped[kp, g][:, u * 2 * GROUP : (u + 1) * 2 * GROUP],
+            )
+
+        def logit_passes(out, g, t, c, first, width):
+            words, base = x_codes[c]
+            days = slice(t * P, (t + 1) * P)
+            customer = c * CHUNK + first
+            for kp in range(PASSES):
+                nc.tensor.matmul_mx(
+                    out=out,
+                    lhsT=w_codes[kp, g][:, days].bitcast(FP8X4),
+                    lhsT_scale=w_planes[kp, g][:, days],
+                    rhs=words[:, kp, base + first : base + first + width].bitcast(FP8X4),
+                    rhs_scale=x_plane[:, kp, customer : customer + width],
+                    start=(kp == 0),
+                    stop=(kp == PASSES - 1),
+                )
+
+        tanh_tiles = {}
+
+        tanh_banks = {}
+
+        def tanh_passes(c, g, u):
+            bank = act_banks.tile([P, 2, CHUNK], F32, name="act_bank")
+            tanh_banks[c, g, u] = bank
+            for e in range(2):
+                logit_passes(bank[:, e, :], g, 2 * u + e, c, 0, CHUNK)
+
+        def tanh_read(c, g, u):
+            if (c, g) not in tanh_tiles:
+                tanh_tiles[c, g] = tanh_pool.tile([P, 2, CHUNK, 2], F32, name="tanh")
+            nc.scalar.activation(
+                out=tanh_tiles[c, g][:, u],
+                in_=tanh_banks[c, g, u][:].rearrange("p e n -> p n e"),
+                func=ACT.Tanh,
+                scale=0.5,
+            )
+
+        def tanh_half(c, g, u):
+            tanh_passes(c, g, u)
+            tanh_read(c, g, u)
+
+        for kp in range(PASSES):
+            group_w(kp, 0, 0, False)
+            group_w(kp, 0, 1, False)
+            group_w(kp, 0, 2, True)
+            group_w(kp, 0, 3, True)
+            if kp == 1:
+                quantize_w(0, 0, 1)
+            quantize_w(kp, 0, 0)
+        quantize_w(1, 0, 1)
+
+        first_chunks = FIRST_TILES // 2
+        for c, u in [(0, 0), (1, 0), (0, 1), (1, 1)] + [(c, u) for c in range(2, first_chunks) for u in range(2)]:
+            tanh_half(c, 0, u)
+
+        for t in range(PACK):
+            group_w(0, 1, t, False)
+        group_w(1, 1, 0, False)
+        quantize_w(0, 1, 0)
+        group_w(1, 1, 1, False)
+        quantize_w(0, 1, 1)
+        group_w(1, 1, 2, False)
+        quantize_w(1, 1, 0)
+        group_w(1, 1, 3, False)
+
+        nc.vector.tensor_scalar(
+            out=vec_rows[0:4, :].rearrange("p (t c i) -> p t c i", t=PACK, i=4),
+            in0=vec_raw[0:4, :].rearrange("p (c t i) -> p t c i", t=PACK, i=4),
+            scalar1=-1.0,
+            scalar2=None,
+            op0=ALU.mult,
+        )
+        nc.vector.tensor_scalar(out=vec_rows[32:36, :], in0=vec_raw[32:36, :], scalar1=-1.0, scalar2=None, op0=ALU.mult)
+        nc.vector.tensor_copy(out=vec_rows[64:65, :], in_=vec_raw[64:65, :])
+        quantize_w(1, 1, 1)
+        a_raw = [load_rows(a, kp, slice(0, J)) for kp in range(PASSES)]
+        cum_raw = keep.tile([P, PASSES, T // 2], I32)
+        nc.sync.dma_start(out=cum_raw[:], in_=cum_words.rearrange("g p n -> p g n").bitcast(I32))
+        load_scale_rows(nc.sync, cum_plane_raw, cum_scales)
+        load_x(*X_LOADS[4])
+
+        a_codes = keep.tile([P, PASSES, J], U32, align_bytes=64)
+        a_plane = keep.tile([P, PASSES, J], U8, align_bytes=64)
+        a_grouped = []
+        for kp in range(PASSES):
+            grouped = stage.tile([P, GROUP * PACK], BF16, name="grouped", align_bytes=64)
+            nc.vector.tensor_copy(
+                out=grouped[:].rearrange("p (c i j) -> p c j i", i=4, j=PACK),
+                in_=a_raw[kp][:].rearrange("p j (c i) -> p c j i", i=4),
+            )
+            a_grouped.append(grouped)
+
+        const_bank = const_banks.tile([P, 2, PACK, P], BF16, name="const_bank")
+        for t in range(PACK):
+            nc.tensor.transpose(const_bank[:, 0, t, :], vec_rows[:, t * P : (t + 1) * P], identity_bf16[:])
+
+        for c in range(first_chunks):
+            for u in range(2):
+                tanh_half(c, 1, u)
+
+        nc.vector.quantize_mx(out=a_codes[:, 0, :].bitcast(FP8X4), scales=a_plane[:, 0, :], in_=a_grouped[0][:])
+        nc.vector.quantize_mx(out=a_codes[:, 1, :].bitcast(FP8X4), scales=a_plane[:, 1, :], in_=a_grouped[1][:])
+
+        cum_codes = keep.tile([P, PASSES * T * 2], U8, align_bytes=64)
+        cum_plane = keep.tile([P, PASSES * T], U8, align_bytes=64)
+        nc.vector.tensor_copy(
+            out=cum_codes[:].bitcast(I32).rearrange("p (k t c i) -> p k t c i", t=PACK, c=32, i=2),
+            in_=cum_raw[:].rearrange("p k (g c t i) -> p (k g) t c i", t=PACK, c=32, i=2),
+        )
+        nc.vector.tensor_copy(
+            out=cum_plane[:].bitcast(I32).rearrange("p (k t c) -> p k t c", t=PACK, c=32),
+            in_=cum_plane_raw[:].rearrange("p k n -> p (k n)").bitcast(I32).rearrange("p (k c t) -> p k t c", t=PACK, c=32),
+        )
+
+        neg_season = keep.tile([P, DAY_GROUPS, PACK], F32)
+        neg_lead = keep.tile([P, DAY_GROUPS, PACK], F32)
+        neg_pace = keep.tile([P, 4, PACK], F32)
+        by_row = const_bank[:, 0].rearrange("p t r -> p r t")
+        value_cols = keep.tile([P, PACK], BF16)
+        nc.vector.tensor_copy(out=value_cols[:], in_=by_row[:, 64, :])
+        nc.vector.tensor_copy(out=neg_lead[:], in_=by_row[:, 2:4, :])
+        nc.vector.tensor_copy(out=neg_season[:], in_=by_row[:, 0:2, :])
+        nc.vector.tensor_copy(out=neg_pace[:], in_=by_row[:, 32:36, :])
+
+        for t in range(PACK):
+            nc.tensor.transpose(const_bank[:, 1, t, :], value_cols[:, t : t + 1].to_broadcast([P, P]), identity_bf16[:])
+        value_psum = const_bank[:, 1].rearrange("p t n -> p (t n)")
+        expo_codes = keep.tile([P, DAY_GROUPS, J], U32, align_bytes=64)
+        expo_plane = keep.tile([P, DAY_GROUPS, J], U8, align_bytes=64)
+        expo_grouped = []
+
+        def quantize_expo(g):
+            nc.vector.quantize_mx(
+                out=expo_codes[:, g, :].bitcast(FP8X4), scales=expo_plane[:, g, :], in_=expo_grouped[g][:]
+            )
+
+        expo_banks = {}
+
+        def expo_passes(i):
+            g, h = divmod(i, J // P)
+            bank = vec_banks.tile([P, PACK, P], F32, name="vec_bank")
+            expo_banks[i] = bank
+            horizons = slice(h * P, (h + 1) * P)
+            for t in range(PACK):
+                for kp in range(PASSES):
+                    slot = (kp * DAY_GROUPS + g) * PACK + t
+                    nc.tensor.matmul_mx(
+                        out=bank[:, t, :],
+                        lhsT=cum_codes[:, slot * 2 * P : (slot + 1) * 2 * P].bitcast(FP4X4),
+                        lhsT_scale=cum_plane[:, slot * P : (slot + 1) * P],
+                        rhs=a_codes[:, kp, horizons].bitcast(FP8X4),
+                        rhs_scale=a_plane[:, kp, horizons],
+                        start=(kp == 0),
+                        stop=(kp == PASSES - 1),
+                    )
+
+        def add_lead(i):
+            g, h = divmod(i, J // P)
+            if h == 0:
+                expo_grouped.append(stage.tile([P, GROUP * PACK], BF16, name="grouped", align_bytes=64))
+            nc.vector.tensor_tensor(
+                out=expo_grouped[g][:, h * GROUP : (h + 1) * GROUP].rearrange("p (n t) -> p n t", t=PACK),
+                in0=expo_banks[i][:].rearrange("p t n -> p n t"),
+                in1=neg_lead[:, g, :].unsqueeze(1).to_broadcast([P, P, PACK]),
+                op=ALU.subtract,
+            )
+
+        ln_tiles, again_banks, loss_grouped = {}, {}, {}
+        loss_codes = keep.tile([P, TILES, DAY_GROUPS * P], U32, align_bytes=64)
+        loss_plane = keep.tile([P, TILES, DAY_GROUPS * P], U8, align_bytes=64)
+
+        def log_tile(m):
+            c, h = divmod(m, 2)
+            ln_tiles[m] = ln_pool.tile([P, DAY_GROUPS, GROUP], F32, name="ln")
+            for g in range(DAY_GROUPS):
+                nc.scalar.activation(
+                    out=ln_tiles[m][:, g, :].rearrange("p (n u e) -> p n u e", u=2, e=2),
+                    in_=tanh_tiles[c, g][:, :, h * P : (h + 1) * P, :].rearrange("p u n e -> p n u e"),
+                    func=ACT.Ln,
+                    scale=0.5,
+                    bias=0.5,
+                )
+
+        def logits_again(m, g):
+            c, h = divmod(m, 2)
+            bank = vec_banks.tile([P, PACK, P], F32, name="vec_bank")
+            for t in range(PACK):
+                logit_passes(bank[:, t, :], g, t, c, h * P, P)
+            again_banks[m, g] = bank
+
+        def bound_half(m, g):
+            logs = ln_tiles[m][:, g, :].rearrange("p (n t) -> p n t", t=PACK)
+            nc.vector.scalar_tensor_tensor(
+                out=logs,
+                in0=logs,
+                scalar=-SOFTPLUS_CAP,
+                in1=again_banks[m, g][:].rearrange("p t n -> p n t"),
+                op0=ALU.max,
+                op1=ALU.min,
+            )
+
+        def season_half(m, g):
+            c, h = divmod(m, 2)
+            if c not in loss_grouped:
+                loss_grouped[c] = stage.tile([P, 2, DAY_GROUPS, GROUP], BF16, name="loss_grouped", bufs=2, align_bytes=64)
+            dst = loss_grouped[c][:, h, g, :].rearrange("p (n t) -> p n t", t=PACK)
+            src = ln_tiles[m][:, g, :].rearrange("p (n t) -> p n t", t=PACK)
+            if SPLIT[2 * m + g] == "G":
+                factors = neg_season[:, g, :].unsqueeze(1).to_broadcast([P, P, PACK])
+                nc.gpsimd.tensor_tensor(out=dst, in0=src, in1=factors, op=ALU.mult)
+            else:
+                factors = by_row[:, g, :].unsqueeze(1).to_broadcast([P, P, PACK])
+                nc.vector.tensor_tensor(out=dst, in0=src, in1=factors, op=ALU.mult)
+
+        def quantize_loss(first, last):
+            c, h = divmod(first, 2)
+            nc.vector.quantize_mx(
+                out=loss_codes[:, first:last, :].rearrange("p m n -> p (m n)").bitcast(FP8X4),
+                scales=loss_plane[:, first:last, :].rearrange("p m n -> p (m n)"),
+                in_=loss_grouped[c][:, h : h + last - first].rearrange("p h g n -> p (h g n)"),
+            )
+
+        survival, y_tiles, y_pairs, y_grouped = {}, {}, {}, {}
+        y_plane = keep.tile([P, B], U8, align_bytes=64)
+
+        def survive(m):
+            bank = act_banks.tile([P, J], F32, name="act_bank")
+            for g in range(DAY_GROUPS):
+                nc.tensor.matmul_mx(
+                    out=bank[:],
+                    lhsT=loss_codes[:, m, g * P : (g + 1) * P].bitcast(FP8X4),
+                    lhsT_scale=loss_plane[:, m, g * P : (g + 1) * P],
+                    rhs=expo_codes[:, g, :].bitcast(FP8X4),
+                    rhs_scale=expo_plane[:, g, :],
+                    start=(g == 0),
+                    stop=(g == DAY_GROUPS - 1),
+                )
+            survival[m] = y_pool.tile([P, J], F32, name="survival", bufs=8)
+            pace_col = neg_pace[:].rearrange("p r t -> p (r t)")[:, m : m + 1]
+            nc.scalar.activation(out=survival[m][:], in_=bank[:], func=ACT.Exp, scale=pace_col)
+
+        def weigh(m):
+            y_tiles[m] = y_pool.tile([P, J], F32, name="y")
+            nc.vector.tensor_tensor(out=y_tiles[m][:], in0=survival[m][:], in1=value_psum, op=ALU.mult)
+            nc.sync.dma_start(out=out_0[m * P : (m + 1) * P, :], in_=y_tiles[m][:])
+
+        def round_y(m):
+            y_pairs[m] = y_pool.tile([P, J], BF16, name="y_pairs", bufs=8)
+            dst = y_pairs[m][:].rearrange("p (u n e) -> p u n e", u=2, e=2)
+            src = y_tiles[m][:].rearrange("p (n u e) -> p u n e", u=2, e=2)
+            if ROUND_ON[m] == "V":
+                nc.vector.tensor_copy(out=dst, in_=src)
+            elif ROUND_ON[m] == "G":
+                nc.gpsimd.tensor_scalar(out=dst, in0=src, scalar1=1.0, scalar2=0.0, op0=ALU.mult, op1=ALU.add)
+            else:
+                nc.scalar.copy(out=dst, in_=src)
+
+        def turn_y(c):
+            bank = act_banks.tile([P, 2, 2, P], F32, name="act_bank")
+            for h in range(2):
+                words = y_pairs[2 * c + h][:].bitcast(F32)
+                for u in range(2):
+                    nc.tensor.transpose(bank[:, h, u, :], words[:, u * P : (u + 1) * P], identity[:])
+            y_grouped[c] = stage.tile([P, CHUNK * PACK], BF16, name="y_grouped", align_bytes=64)
+            nc.scalar.copy(
+                out=y_grouped[c][:].bitcast(F32).rearrange("p (h n u) -> p h n u", h=2, u=2),
+                in_=bank[:].rearrange("p h u n -> p h n u"),
+            )
+
+        def quantize_y(c):
+            codes = stage.tile([P, CHUNK], U32, name="y_codes", align_bytes=64)
+            customers = slice(c * CHUNK, (c + 1) * CHUNK)
+            nc.vector.quantize_mx(out=codes[:].bitcast(FP8X4), scales=y_plane[:, customers], in_=y_grouped[c][:])
+            dst = out_1[0].rearrange("p n t -> p (n t)")[:, c * CHUNK * PACK : (c + 1) * CHUNK * PACK]
+            nc.sync.dma_start(out=dst.bitcast(I32), in_=codes[:].bitcast(I32))
+
+        def store_scale_rows(customers, queues):
+            for q in range(4):
+                queues[q % len(queues)].dma_start(
+                    out=out_2[0, 4 * q : 4 * q + 4, customers].bitcast(I32),
+                    in_=y_plane[32 * q : 32 * q + 4, customers].bitcast(I32),
+                )
+
+        for m in range(LN_AHEAD):
+            log_tile(m)
+        for i in range(EXPO_FIRST):
+            expo_passes(i)
+            add_lead(i)
+        halves = [(m, g) for m in range(TILES) for g in range(DAY_GROUPS)]
+        for half in halves[:VEC_BANKS - 1]:
+            logits_again(*half)
+        later_halves = [
+            (c, g, u) for c in range(first_chunks, TILES // 2) for g in range(DAY_GROUPS) for u in range(2)
+        ]
+        last_step = max(QY_STEP)
+        for s in range(last_step + 1):
+            if s + LN_AHEAD < FIRST_TILES:
+                log_tile(s + LN_AHEAD)
+            for g in range(DAY_GROUPS):
+                i = 2 * s + g
+                if i + VEC_BANKS - 1 < len(halves):
+                    logits_again(*halves[i + VEC_BANKS - 1])
+                if i < len(halves):
+                    bound_half(*halves[i])
+                if g == 1:
+                    if s % 2 == 0 and 2 <= s < TILES:
+                        quantize_loss(s - 2, s)
+                    if s == TILES - 1:
+                        quantize_loss(s - 1, s)
+                    if s < DAY_GROUPS:
+                        quantize_expo(s)
+                    for c in range(TILES // 2):
+                        if QY_STEP[c] == s:
+                            quantize_y(c)
+                if i < len(halves) and SPLIT[i] == "G":
+                    season_half(*halves[i])
+                if 1 <= i <= len(halves) and SPLIT[i - 1] != "G":
+                    season_half(*halves[i - 1])
+            if s == TILES:
+                quantize_loss(s - 1, s)
+            for m in range(TILES):
+                if WEIGH_STEP[m] == s:
+                    weigh(m)
+            for i, half in enumerate(later_halves):
+                if TANH_MM[i] == s:
+                    tanh_passes(*half)
+                if TANH_RD[i] == s:
+                    tanh_read(*half)
+            for m in range(TILES):
+                if EXP_STEP[m] == s:
+                    survive(m)
+            if s == LN_STEP:
+                for m in range(FIRST_TILES, TILES):
+                    log_tile(m)
+            for c in range(TILES // 2):
+                if TURN_STEP[c] == s:
+                    turn_y(c)
+            for m in range(TILES):
+                if ROUND_STEP[m] == s:
+                    round_y(m)
+        store_scale_rows(slice(0, B), [nc.sync, nc.scalar])

@@ -15,45 +15,39 @@ FP8X4 = mybir.dt.float8_e4m3fn_x4
 FP4X4 = mybir.dt.float4_e2m1fn_x4
 ACT = mybir.ActivationFunctionType
 ALU = mybir.AluOpType
+ENGINE = mybir.EngineType
 
 P = 128
 PACK = 4
+RUN = 4
 GROUP = P * PACK
 PASSES = K // GROUP
 DAY_GROUPS = T // GROUP
 TILES = B // P
 CHUNK = 2 * P
-BANK = 512
+CHUNKS = B // CHUNK
+
 SOFTPLUS_CAP = 8.0
 
+SEASON_ROW, LEAD_ROW, PACE_ROW, VALUE_ROW = 0, 2, 32, 64
+
+VECTOR_BANKS = 3
+SCALAR_BANKS = 4
+
 FIRST_TILES = 10
-LN_AHEAD = 7
-EARLY_TILES = 8
-EARLY_STEP = 5
-LN_STEP = 8
+LOG_AHEAD = 7
+LAST_FIRST_LOG = FIRST_TILES - 1 - LOG_AHEAD
+LATER_LOG_STEP = FIRST_TILES - 2
+EARLY_TILES = 4
+EARLY_STEP = 4
 LATE_STEP = 12
-VEC_BANKS = 3
-EXPO_FIRST = 8
-X_LOADS = ((0, 1), (1, 2), (2, 3), (3, 5), (5, 8))
 LAST_PAIR = TILES - 2
 
-
-def loss_ready(m):
-    return m + 1 if m >= LAST_PAIR else m // 2 * 2 + 2
-
-
-EXP_STEP = [
-    EARLY_STEP + m // 2 if m < EARLY_TILES else max(loss_ready(m), LATE_STEP + (m - EARLY_TILES) // 2)
-    for m in range(TILES)
-]
+EXP_STEP = [EARLY_STEP + m // 2 if m < EARLY_TILES else LATE_STEP + (m - EARLY_TILES) // 2 for m in range(TILES)]
 WEIGH_STEP = [s + 1 for s in EXP_STEP]
-ROUND_STEP = WEIGH_STEP
-TURN_STEP = [max(LATE_STEP + 1 + c // 2, EXP_STEP[2 * c + 1] + 2) for c in range(TILES // 2)]
-QY_STEP = [s + 1 for s in TURN_STEP]
-TANH_MM = [i // 2 if i < 4 else i // 2 + 1 for i in range(12)]
-TANH_RD = [max(2, s) for s in TANH_MM]
-SPLIT = "VG" * (TILES - 1) + "VV"
-ROUND_ON = "G" * EARLY_TILES + "S" * (LAST_PAIR - EARLY_TILES) + "VV"
+PLANE_RANGES = [(m, m + 2) for m in range(0, LAST_PAIR, 2)] + [(m, m + 1) for m in range(LAST_PAIR, TILES)]
+TURN_STEP = [max(LATE_STEP + 1 + r // 2, WEIGH_STEP[last - 1] + 1) for r, (first, last) in enumerate(PLANE_RANGES)]
+PLANE_STEP = [s + 1 + (s + 1) % 2 if s + 1 < TILES else s + 1 for s in TURN_STEP]
 
 
 def tile_churn_survival_horizons_k4_kernel(
@@ -64,13 +58,13 @@ def tile_churn_survival_horizons_k4_kernel(
         keep = ctx.enter_context(tc.tile_pool(name="keep", bufs=1))
         raw_pool = ctx.enter_context(tc.tile_pool(name="raw", bufs=4))
         stage = ctx.enter_context(tc.tile_pool(name="stage", bufs=3))
-        tanh_pool = ctx.enter_context(tc.tile_pool(name="tanh", bufs=max(FIRST_TILES, TILES - FIRST_TILES)))
-        ln_pool = ctx.enter_context(tc.tile_pool(name="ln", bufs=LN_AHEAD + 1))
+        tanh_pool = ctx.enter_context(tc.tile_pool(name="tanh", bufs=FIRST_TILES))
+        log_pool = ctx.enter_context(tc.tile_pool(name="log", bufs=LOG_AHEAD + 2))
         y_pool = ctx.enter_context(tc.tile_pool(name="y", bufs=5))
-        vec_banks = ctx.enter_context(tc.psum_pool(name="vec_banks", bufs=VEC_BANKS))
-        act_banks = ctx.enter_context(tc.psum_pool(name="act_banks", bufs=7 - VEC_BANKS))
+        vector_banks = ctx.enter_context(tc.psum_pool(name="vector_banks", bufs=VECTOR_BANKS))
+        scalar_banks = ctx.enter_context(tc.psum_pool(name="scalar_banks", bufs=SCALAR_BANKS))
         const_banks = ctx.enter_context(tc.psum_pool(name="const_banks", bufs=1))
-        ctx.enter_context(tc.manual_schedule(engines={mybir.EngineType.Activation, mybir.EngineType.DVE, mybir.EngineType.SP}))
+        ctx.enter_context(tc.manual_schedule(engines={ENGINE.Activation, ENGINE.DVE, ENGINE.SP}))
 
         def load_rows(src, kp, cols):
             raw = raw_pool.tile([P, PACK, GROUP], BF16, name="raw")
@@ -79,9 +73,9 @@ def tile_churn_survival_horizons_k4_kernel(
             )
             return raw
 
-        def load_scale_rows(queue, plane, src):
+        def load_scale_rows(plane, src):
             for q in range(4):
-                queue.dma_start(
+                nc.sync.dma_start(
                     out=plane[32 * q : 32 * q + 4, :, :].bitcast(I32),
                     in_=src[:, 4 * q : 4 * q + 4, :].rearrange("g r n -> r g n").bitcast(I32),
                 )
@@ -106,29 +100,30 @@ def tile_churn_survival_horizons_k4_kernel(
         identity_bf16 = keep.tile([P, P], BF16)
         make_identity(nc, identity_bf16[:])
 
+        first_chunks = FIRST_TILES // 2
         w_raw = {}
         w_raw[0, 0] = load_rows(w, 0, slice(0, GROUP))
         w_raw[1, 0] = load_rows(w, 1, slice(0, GROUP))
-        load_scale_rows(nc.sync, x_plane, x_scales)
-        load_x(*X_LOADS[0])
-        load_x(*X_LOADS[1])
+        load_scale_rows(x_plane, x_scales)
+        load_x(1, 2)
+        load_x(2, 3)
         w_raw[0, 1] = load_rows(w, 0, slice(GROUP, 2 * GROUP))
-        load_x(*X_LOADS[2])
+        load_x(3, 4)
         w_raw[1, 1] = load_rows(w, 1, slice(GROUP, 2 * GROUP))
-        load_x(*X_LOADS[3])
+        load_x(4, first_chunks)
+        load_x(0, 1)
         vec_raw = keep.tile([P, GROUP], BF16)
-        nc.sync.dma_start(out=vec_raw[0:2, :], in_=season.rearrange("(g n) -> g n", n=GROUP))
-        nc.sync.dma_start(out=vec_raw[2:4, :], in_=lead.rearrange("(g n) -> g n", n=GROUP))
-        nc.sync.dma_start(out=vec_raw[32:36, :], in_=pace.rearrange("(g n) -> g n", n=GROUP))
-        nc.sync.dma_start(out=vec_raw[64:65, :], in_=value.rearrange("(g n) -> g n", n=GROUP))
+        for vec, row in ((season, SEASON_ROW), (lead, LEAD_ROW), (pace, PACE_ROW), (value, VALUE_ROW)):
+            rows = vec.rearrange("(r n) -> r n", n=GROUP)
+            nc.sync.dma_start(out=vec_raw[row : row + rows.shape[0], :], in_=rows)
 
         w_codes, w_planes, w_grouped = {}, {}, {}
 
         def group_w(kp, g, t, on_scalar):
             if (kp, g) not in w_grouped:
                 w_grouped[kp, g] = stage.tile([P, GROUP * PACK], BF16, name="grouped", align_bytes=64)
-            dst = w_grouped[kp, g][:, t * GROUP : (t + 1) * GROUP].rearrange("p (c i j) -> p c j i", i=4, j=PACK)
-            src = w_raw[kp, g][:].rearrange("p j (c t i) -> p t c j i", t=PACK, i=4)[:, t]
+            dst = w_grouped[kp, g][:, t * GROUP : (t + 1) * GROUP].rearrange("p (c i j) -> p c j i", i=RUN, j=PACK)
+            src = w_raw[kp, g][:].rearrange("p j (c t i) -> p t c j i", t=PACK, i=RUN)[:, t]
             if on_scalar:
                 nc.scalar.activation(out=dst, in_=src, func=ACT.Copy, scale=-1.0)
             else:
@@ -160,15 +155,12 @@ def tile_churn_survival_horizons_k4_kernel(
                     stop=(kp == PASSES - 1),
                 )
 
-        tanh_tiles = {}
-
-        tanh_banks = {}
+        tanh_tiles, tanh_banks, logit_banks = {}, {}, {}
 
         def tanh_passes(c, g, u):
-            bank = act_banks.tile([P, 2, CHUNK], F32, name="act_bank")
-            tanh_banks[c, g, u] = bank
+            tanh_banks[c, g, u] = scalar_banks.tile([P, 2, CHUNK], F32, name="scalar_bank")
             for e in range(2):
-                logit_passes(bank[:, e, :], g, 2 * u + e, c, 0, CHUNK)
+                logit_passes(tanh_banks[c, g, u][:, e, :], g, 2 * u + e, c, 0, CHUNK)
 
         def tanh_read(c, g, u):
             if (c, g) not in tanh_tiles:
@@ -180,23 +172,30 @@ def tile_churn_survival_horizons_k4_kernel(
                 scale=0.5,
             )
 
-        def tanh_half(c, g, u):
-            tanh_passes(c, g, u)
-            tanh_read(c, g, u)
+        def tanh_kept(m, g):
+            if (0, g) not in tanh_tiles:
+                tanh_tiles[0, g] = tanh_pool.tile([P, 2, P, PACK], F32, name="tanh")
+            logit_banks[m, g] = scalar_banks.tile([P, PACK, P], F32, name="scalar_bank")
+            for t in range(PACK):
+                logit_passes(logit_banks[m, g][:, t, :], g, t, 0, m * P, P)
+            nc.scalar.activation(
+                out=tanh_tiles[0, g][:, m],
+                in_=logit_banks[m, g][:].rearrange("p t n -> p n t"),
+                func=ACT.Tanh,
+                scale=0.5,
+            )
 
         for kp in range(PASSES):
-            group_w(kp, 0, 0, False)
-            group_w(kp, 0, 1, False)
-            group_w(kp, 0, 2, True)
-            group_w(kp, 0, 3, True)
+            for t in range(PACK):
+                group_w(kp, 0, t, on_scalar=(t >= 2))
             if kp == 1:
                 quantize_w(0, 0, 1)
             quantize_w(kp, 0, 0)
         quantize_w(1, 0, 1)
 
-        first_chunks = FIRST_TILES // 2
-        for c, u in [(0, 0), (1, 0), (0, 1), (1, 1)] + [(c, u) for c in range(2, first_chunks) for u in range(2)]:
-            tanh_half(c, 0, u)
+        for c, u in [(1, 0), (2, 0), (1, 1), (2, 1)] + [(c, u) for c in range(3, first_chunks) for u in range(2)]:
+            tanh_passes(c, 0, u)
+            tanh_read(c, 0, u)
 
         for t in range(PACK):
             group_w(0, 1, t, False)
@@ -208,21 +207,27 @@ def tile_churn_survival_horizons_k4_kernel(
         quantize_w(1, 1, 0)
         group_w(1, 1, 3, False)
 
+        by_day = slice(SEASON_ROW, LEAD_ROW + DAY_GROUPS)
+        pace_rows = slice(PACE_ROW, PACE_ROW + B // GROUP)
+        value_row = slice(VALUE_ROW, VALUE_ROW + 1)
         nc.vector.tensor_scalar(
-            out=vec_rows[0:4, :].rearrange("p (t c i) -> p t c i", t=PACK, i=4),
-            in0=vec_raw[0:4, :].rearrange("p (c t i) -> p t c i", t=PACK, i=4),
+            out=vec_rows[by_day, :].rearrange("p (t c i) -> p t c i", t=PACK, i=RUN),
+            in0=vec_raw[by_day, :].rearrange("p (c t i) -> p t c i", t=PACK, i=RUN),
             scalar1=-1.0,
             scalar2=None,
             op0=ALU.mult,
         )
-        nc.vector.tensor_scalar(out=vec_rows[32:36, :], in0=vec_raw[32:36, :], scalar1=-1.0, scalar2=None, op0=ALU.mult)
-        nc.vector.tensor_copy(out=vec_rows[64:65, :], in_=vec_raw[64:65, :])
         quantize_w(1, 1, 1)
+        nc.vector.tensor_scalar(
+            out=vec_rows[pace_rows, :], in0=vec_raw[pace_rows, :], scalar1=-1.0, scalar2=None, op0=ALU.mult
+        )
+        nc.vector.tensor_copy(out=vec_rows[value_row, :], in_=vec_raw[value_row, :])
+
         a_raw = [load_rows(a, kp, slice(0, J)) for kp in range(PASSES)]
         cum_raw = keep.tile([P, PASSES, T // 2], I32)
         nc.sync.dma_start(out=cum_raw[:], in_=cum_words.rearrange("g p n -> p g n").bitcast(I32))
-        load_scale_rows(nc.sync, cum_plane_raw, cum_scales)
-        load_x(*X_LOADS[4])
+        load_scale_rows(cum_plane_raw, cum_scales)
+        load_x(first_chunks, CHUNKS)
 
         a_codes = keep.tile([P, PASSES, J], U32, align_bytes=64)
         a_plane = keep.tile([P, PASSES, J], U8, align_bytes=64)
@@ -230,8 +235,8 @@ def tile_churn_survival_horizons_k4_kernel(
         for kp in range(PASSES):
             grouped = stage.tile([P, GROUP * PACK], BF16, name="grouped", align_bytes=64)
             nc.vector.tensor_copy(
-                out=grouped[:].rearrange("p (c i j) -> p c j i", i=4, j=PACK),
-                in_=a_raw[kp][:].rearrange("p j (c i) -> p c j i", i=4),
+                out=grouped[:].rearrange("p (c i j) -> p c j i", i=RUN, j=PACK),
+                in_=a_raw[kp][:].rearrange("p j (c i) -> p c j i", i=RUN),
             )
             a_grouped.append(grouped)
 
@@ -239,88 +244,103 @@ def tile_churn_survival_horizons_k4_kernel(
         for t in range(PACK):
             nc.tensor.transpose(const_bank[:, 0, t, :], vec_rows[:, t * P : (t + 1) * P], identity_bf16[:])
 
-        for c in range(first_chunks):
+        for c in range(1, first_chunks):
             for u in range(2):
-                tanh_half(c, 1, u)
+                tanh_passes(c, 1, u)
+                tanh_read(c, 1, u)
+        for m in range(2):
+            for g in range(DAY_GROUPS):
+                tanh_kept(m, g)
 
-        nc.vector.quantize_mx(out=a_codes[:, 0, :].bitcast(FP8X4), scales=a_plane[:, 0, :], in_=a_grouped[0][:])
-        nc.vector.quantize_mx(out=a_codes[:, 1, :].bitcast(FP8X4), scales=a_plane[:, 1, :], in_=a_grouped[1][:])
+        for kp in range(PASSES):
+            nc.vector.quantize_mx(
+                out=a_codes[:, kp, :].bitcast(FP8X4), scales=a_plane[:, kp, :], in_=a_grouped[kp][:]
+            )
 
+        runs = P // RUN
         cum_codes = keep.tile([P, PASSES * T * 2], U8, align_bytes=64)
         cum_plane = keep.tile([P, PASSES * T], U8, align_bytes=64)
         nc.vector.tensor_copy(
-            out=cum_codes[:].bitcast(I32).rearrange("p (k t c i) -> p k t c i", t=PACK, c=32, i=2),
-            in_=cum_raw[:].rearrange("p k (g c t i) -> p (k g) t c i", t=PACK, c=32, i=2),
+            out=cum_codes[:].bitcast(I32).rearrange("p (k t c i) -> p k t c i", t=PACK, c=runs, i=2),
+            in_=cum_raw[:].rearrange("p k (g c t i) -> p (k g) t c i", t=PACK, c=runs, i=2),
         )
         nc.vector.tensor_copy(
-            out=cum_plane[:].bitcast(I32).rearrange("p (k t c) -> p k t c", t=PACK, c=32),
-            in_=cum_plane_raw[:].rearrange("p k n -> p (k n)").bitcast(I32).rearrange("p (k c t) -> p k t c", t=PACK, c=32),
+            out=cum_plane[:].bitcast(I32).rearrange("p (k t c) -> p k t c", t=PACK, c=runs),
+            in_=cum_plane_raw[:]
+            .rearrange("p k n -> p (k n)")
+            .bitcast(I32)
+            .rearrange("p (k c t) -> p k t c", t=PACK, c=runs),
         )
 
-        neg_season = keep.tile([P, DAY_GROUPS, PACK], F32)
-        neg_lead = keep.tile([P, DAY_GROUPS, PACK], F32)
-        neg_pace = keep.tile([P, 4, PACK], F32)
         by_row = const_bank[:, 0].rearrange("p t r -> p r t")
+        neg_lead = keep.tile([P, DAY_GROUPS, PACK], F32)
+        neg_pace = keep.tile([P, B // GROUP, PACK], F32)
         value_cols = keep.tile([P, PACK], BF16)
-        nc.vector.tensor_copy(out=value_cols[:], in_=by_row[:, 64, :])
-        nc.vector.tensor_copy(out=neg_lead[:], in_=by_row[:, 2:4, :])
-        nc.vector.tensor_copy(out=neg_season[:], in_=by_row[:, 0:2, :])
-        nc.vector.tensor_copy(out=neg_pace[:], in_=by_row[:, 32:36, :])
+        nc.vector.tensor_copy(out=value_cols[:], in_=by_row[:, VALUE_ROW, :])
+        nc.vector.tensor_copy(out=neg_lead[:], in_=by_row[:, LEAD_ROW : LEAD_ROW + DAY_GROUPS, :])
+        nc.vector.tensor_copy(out=neg_pace[:], in_=by_row[:, pace_rows, :])
+
+        def neg_season(g):
+            return by_row[:, SEASON_ROW + g, :].unsqueeze(1).to_broadcast([P, P, PACK])
+
+        season_words = keep.tile([P, GROUP], BF16)
+        nc.vector.tensor_copy(out=season_words[:].rearrange("p (n t) -> p n t", t=PACK), in_=neg_season(0))
 
         for t in range(PACK):
-            nc.tensor.transpose(const_bank[:, 1, t, :], value_cols[:, t : t + 1].to_broadcast([P, P]), identity_bf16[:])
-        value_psum = const_bank[:, 1].rearrange("p t n -> p (t n)")
+            nc.tensor.transpose(
+                const_bank[:, 1, t, :], value_cols[:, t : t + 1].to_broadcast([P, P]), identity_bf16[:]
+            )
+        value_rows = const_bank[:, 1].rearrange("p t n -> p (t n)")
+
         expo_codes = keep.tile([P, DAY_GROUPS, J], U32, align_bytes=64)
         expo_plane = keep.tile([P, DAY_GROUPS, J], U8, align_bytes=64)
         expo_grouped = []
+
+        def expo_group(g):
+            grouped = stage.tile([P, GROUP * PACK], BF16, name="grouped", align_bytes=64)
+            expo_grouped.append(grouped)
+            for h in range(J // P):
+                bank = vector_banks.tile([P, PACK, P], F32, name="vector_bank")
+                horizons = slice(h * P, (h + 1) * P)
+                for t in range(PACK):
+                    for kp in range(PASSES):
+                        block = (kp * DAY_GROUPS + g) * PACK + t
+                        nc.tensor.matmul_mx(
+                            out=bank[:, t, :],
+                            lhsT=cum_codes[:, block * 2 * P : (block + 1) * 2 * P].bitcast(FP4X4),
+                            lhsT_scale=cum_plane[:, block * P : (block + 1) * P],
+                            rhs=a_codes[:, kp, horizons].bitcast(FP8X4),
+                            rhs_scale=a_plane[:, kp, horizons],
+                            start=(kp == 0),
+                            stop=(kp == PASSES - 1),
+                        )
+                nc.vector.tensor_tensor(
+                    out=grouped[:, h * GROUP : (h + 1) * GROUP].rearrange("p (n t) -> p n t", t=PACK),
+                    in0=bank[:].rearrange("p t n -> p n t"),
+                    in1=neg_lead[:, g, :].unsqueeze(1).to_broadcast([P, P, PACK]),
+                    op=ALU.subtract,
+                )
 
         def quantize_expo(g):
             nc.vector.quantize_mx(
                 out=expo_codes[:, g, :].bitcast(FP8X4), scales=expo_plane[:, g, :], in_=expo_grouped[g][:]
             )
 
-        expo_banks = {}
-
-        def expo_passes(i):
-            g, h = divmod(i, J // P)
-            bank = vec_banks.tile([P, PACK, P], F32, name="vec_bank")
-            expo_banks[i] = bank
-            horizons = slice(h * P, (h + 1) * P)
-            for t in range(PACK):
-                for kp in range(PASSES):
-                    slot = (kp * DAY_GROUPS + g) * PACK + t
-                    nc.tensor.matmul_mx(
-                        out=bank[:, t, :],
-                        lhsT=cum_codes[:, slot * 2 * P : (slot + 1) * 2 * P].bitcast(FP4X4),
-                        lhsT_scale=cum_plane[:, slot * P : (slot + 1) * P],
-                        rhs=a_codes[:, kp, horizons].bitcast(FP8X4),
-                        rhs_scale=a_plane[:, kp, horizons],
-                        start=(kp == 0),
-                        stop=(kp == PASSES - 1),
-                    )
-
-        def add_lead(i):
-            g, h = divmod(i, J // P)
-            if h == 0:
-                expo_grouped.append(stage.tile([P, GROUP * PACK], BF16, name="grouped", align_bytes=64))
-            nc.vector.tensor_tensor(
-                out=expo_grouped[g][:, h * GROUP : (h + 1) * GROUP].rearrange("p (n t) -> p n t", t=PACK),
-                in0=expo_banks[i][:].rearrange("p t n -> p n t"),
-                in1=neg_lead[:, g, :].unsqueeze(1).to_broadcast([P, P, PACK]),
-                op=ALU.subtract,
-            )
-
-        ln_tiles, again_banks, loss_grouped = {}, {}, {}
+        log_tiles, loss_grouped = {}, {}
         loss_codes = keep.tile([P, TILES, DAY_GROUPS * P], U32, align_bytes=64)
         loss_plane = keep.tile([P, TILES, DAY_GROUPS * P], U8, align_bytes=64)
 
         def log_tile(m):
             c, h = divmod(m, 2)
-            ln_tiles[m] = ln_pool.tile([P, DAY_GROUPS, GROUP], F32, name="ln")
+            log_tiles[m] = log_pool.tile([P, DAY_GROUPS, GROUP], F32, name="log")
             for g in range(DAY_GROUPS):
+                if c == 0:
+                    src = tanh_tiles[c, g][:, h].rearrange("p n (u e) -> p n u e", e=2)
+                else:
+                    src = tanh_tiles[c, g][:, :, h * P : (h + 1) * P, :].rearrange("p u n e -> p n u e")
                 nc.scalar.activation(
-                    out=ln_tiles[m][:, g, :].rearrange("p (n u e) -> p n u e", u=2, e=2),
-                    in_=tanh_tiles[c, g][:, :, h * P : (h + 1) * P, :].rearrange("p u n e -> p n u e"),
+                    out=log_tiles[m][:, g, :].rearrange("p (n u e) -> p n u e", u=2, e=2),
+                    in_=src,
                     func=ACT.Ln,
                     scale=0.5,
                     bias=0.5,
@@ -328,48 +348,51 @@ def tile_churn_survival_horizons_k4_kernel(
 
         def logits_again(m, g):
             c, h = divmod(m, 2)
-            bank = vec_banks.tile([P, PACK, P], F32, name="vec_bank")
+            logit_banks[m, g] = vector_banks.tile([P, PACK, P], F32, name="vector_bank")
             for t in range(PACK):
-                logit_passes(bank[:, t, :], g, t, c, h * P, P)
-            again_banks[m, g] = bank
+                logit_passes(logit_banks[m, g][:, t, :], g, t, c, h * P, P)
 
         def bound_half(m, g):
-            logs = ln_tiles[m][:, g, :].rearrange("p (n t) -> p n t", t=PACK)
+            logs = log_tiles[m][:, g, :].rearrange("p (n t) -> p n t", t=PACK)
             nc.vector.scalar_tensor_tensor(
                 out=logs,
                 in0=logs,
                 scalar=-SOFTPLUS_CAP,
-                in1=again_banks[m, g][:].rearrange("p t n -> p n t"),
+                in1=logit_banks[m, g][:].rearrange("p t n -> p n t"),
                 op0=ALU.max,
                 op1=ALU.min,
             )
 
-        def season_half(m, g):
+        def season_on_gpsimd(m):
             c, h = divmod(m, 2)
-            if c not in loss_grouped:
-                loss_grouped[c] = stage.tile([P, 2, DAY_GROUPS, GROUP], BF16, name="loss_grouped", bufs=2, align_bytes=64)
-            dst = loss_grouped[c][:, h, g, :].rearrange("p (n t) -> p n t", t=PACK)
-            src = ln_tiles[m][:, g, :].rearrange("p (n t) -> p n t", t=PACK)
-            if SPLIT[2 * m + g] == "G":
-                factors = neg_season[:, g, :].unsqueeze(1).to_broadcast([P, P, PACK])
-                nc.gpsimd.tensor_tensor(out=dst, in0=src, in1=factors, op=ALU.mult)
-            else:
-                factors = by_row[:, g, :].unsqueeze(1).to_broadcast([P, P, PACK])
-                nc.vector.tensor_tensor(out=dst, in0=src, in1=factors, op=ALU.mult)
+            if h == 0:
+                loss_grouped[c] = stage.tile([P, 2, T], BF16, name="loss_grouped", bufs=2, align_bytes=64)
+            nc.gpsimd.tensor_tensor(
+                out=loss_grouped[c][:, h, :GROUP], in0=log_tiles[m][:, 0, :], in1=season_words[:], op=ALU.mult
+            )
+
+        def season_on_vector(m):
+            c, h = divmod(m, 2)
+            nc.vector.tensor_tensor(
+                out=loss_grouped[c][:, h, GROUP:].rearrange("p (n t) -> p n t", t=PACK),
+                in0=log_tiles[m][:, 1, :].rearrange("p (n t) -> p n t", t=PACK),
+                in1=neg_season(1),
+                op=ALU.mult,
+            )
 
         def quantize_loss(first, last):
             c, h = divmod(first, 2)
             nc.vector.quantize_mx(
                 out=loss_codes[:, first:last, :].rearrange("p m n -> p (m n)").bitcast(FP8X4),
                 scales=loss_plane[:, first:last, :].rearrange("p m n -> p (m n)"),
-                in_=loss_grouped[c][:, h : h + last - first].rearrange("p h g n -> p (h g n)"),
+                in_=loss_grouped[c][:, h : h + last - first].rearrange("p h n -> p (h n)"),
             )
 
         survival, y_tiles, y_pairs, y_grouped = {}, {}, {}, {}
         y_plane = keep.tile([P, B], U8, align_bytes=64)
 
         def survive(m):
-            bank = act_banks.tile([P, J], F32, name="act_bank")
+            bank = scalar_banks.tile([P, J], F32, name="scalar_bank")
             for g in range(DAY_GROUPS):
                 nc.tensor.matmul_mx(
                     out=bank[:],
@@ -380,107 +403,105 @@ def tile_churn_survival_horizons_k4_kernel(
                     start=(g == 0),
                     stop=(g == DAY_GROUPS - 1),
                 )
-            survival[m] = y_pool.tile([P, J], F32, name="survival", bufs=8)
+            survival[m] = y_pool.tile([P, J], F32, name="survival", bufs=6)
             pace_col = neg_pace[:].rearrange("p r t -> p (r t)")[:, m : m + 1]
             nc.scalar.activation(out=survival[m][:], in_=bank[:], func=ACT.Exp, scale=pace_col)
 
         def weigh(m):
             y_tiles[m] = y_pool.tile([P, J], F32, name="y")
-            nc.vector.tensor_tensor(out=y_tiles[m][:], in0=survival[m][:], in1=value_psum, op=ALU.mult)
+            nc.vector.tensor_tensor(out=y_tiles[m][:], in0=survival[m][:], in1=value_rows, op=ALU.mult)
             nc.sync.dma_start(out=out_0[m * P : (m + 1) * P, :], in_=y_tiles[m][:])
 
         def round_y(m):
             y_pairs[m] = y_pool.tile([P, J], BF16, name="y_pairs", bufs=8)
             dst = y_pairs[m][:].rearrange("p (u n e) -> p u n e", u=2, e=2)
             src = y_tiles[m][:].rearrange("p (n u e) -> p u n e", u=2, e=2)
-            if ROUND_ON[m] == "V":
+            if m >= LAST_PAIR:
                 nc.vector.tensor_copy(out=dst, in_=src)
-            elif ROUND_ON[m] == "G":
-                nc.gpsimd.tensor_scalar(out=dst, in0=src, scalar1=1.0, scalar2=0.0, op0=ALU.mult, op1=ALU.add)
             else:
                 nc.scalar.copy(out=dst, in_=src)
 
-        def turn_y(c):
-            bank = act_banks.tile([P, 2, 2, P], F32, name="act_bank")
-            for h in range(2):
-                words = y_pairs[2 * c + h][:].bitcast(F32)
+        def turn_y(r):
+            first, last = PLANE_RANGES[r]
+            bank = scalar_banks.tile([P, last - first, 2, P], F32, name="scalar_bank")
+            for h in range(last - first):
+                words = y_pairs[first + h][:].bitcast(F32)
                 for u in range(2):
                     nc.tensor.transpose(bank[:, h, u, :], words[:, u * P : (u + 1) * P], identity[:])
-            y_grouped[c] = stage.tile([P, CHUNK * PACK], BF16, name="y_grouped", align_bytes=64)
+            y_grouped[r] = stage.tile([P, (last - first) * GROUP], BF16, name="y_grouped", align_bytes=64)
             nc.scalar.copy(
-                out=y_grouped[c][:].bitcast(F32).rearrange("p (h n u) -> p h n u", h=2, u=2),
+                out=y_grouped[r][:].bitcast(F32).rearrange("p (h n u) -> p h n u", n=P, u=2),
                 in_=bank[:].rearrange("p h u n -> p h n u"),
             )
 
-        def quantize_y(c):
-            codes = stage.tile([P, CHUNK], U32, name="y_codes", align_bytes=64)
-            customers = slice(c * CHUNK, (c + 1) * CHUNK)
-            nc.vector.quantize_mx(out=codes[:].bitcast(FP8X4), scales=y_plane[:, customers], in_=y_grouped[c][:])
-            dst = out_1[0].rearrange("p n t -> p (n t)")[:, c * CHUNK * PACK : (c + 1) * CHUNK * PACK]
+        def quantize_y(r):
+            first, last = PLANE_RANGES[r]
+            codes = stage.tile([P, (last - first) * P], U32, name="y_codes", align_bytes=64)
+            nc.vector.quantize_mx(
+                out=codes[:].bitcast(FP8X4), scales=y_plane[:, first * P : last * P], in_=y_grouped[r][:]
+            )
+            dst = out_1[0].rearrange("p n t -> p (n t)")[:, first * GROUP : last * GROUP]
             nc.sync.dma_start(out=dst.bitcast(I32), in_=codes[:].bitcast(I32))
 
-        def store_scale_rows(customers, queues):
-            for q in range(4):
-                queues[q % len(queues)].dma_start(
-                    out=out_2[0, 4 * q : 4 * q + 4, customers].bitcast(I32),
-                    in_=y_plane[32 * q : 32 * q + 4, customers].bitcast(I32),
-                )
-
-        for m in range(LN_AHEAD):
+        for m in range(LOG_AHEAD):
             log_tile(m)
-        for i in range(EXPO_FIRST):
-            expo_passes(i)
-            add_lead(i)
-        halves = [(m, g) for m in range(TILES) for g in range(DAY_GROUPS)]
-        for half in halves[:VEC_BANKS - 1]:
-            logits_again(*half)
-        later_halves = [
-            (c, g, u) for c in range(first_chunks, TILES // 2) for g in range(DAY_GROUPS) for u in range(2)
-        ]
-        last_step = max(QY_STEP)
-        for s in range(last_step + 1):
-            if s + LN_AHEAD < FIRST_TILES:
-                log_tile(s + LN_AHEAD)
+        for g in range(DAY_GROUPS):
+            expo_group(g)
+
+        later_banks = [(c, g, u) for c in range(first_chunks, CHUNKS) for g in range(DAY_GROUPS) for u in range(2)]
+        for s in range(max(PLANE_STEP) + 1):
+            if s <= LAST_FIRST_LOG:
+                log_tile(s + LOG_AHEAD)
             for g in range(DAY_GROUPS):
-                i = 2 * s + g
-                if i + VEC_BANKS - 1 < len(halves):
-                    logits_again(*halves[i + VEC_BANKS - 1])
-                if i < len(halves):
-                    bound_half(*halves[i])
-                if g == 1:
+                if 2 <= s + 1 < TILES:
+                    logits_again(s + 1, g)
+                if s < TILES:
+                    bound_half(s, g)
+                if g == 0:
                     if s % 2 == 0 and 2 <= s < TILES:
                         quantize_loss(s - 2, s)
-                    if s == TILES - 1:
-                        quantize_loss(s - 1, s)
                     if s < DAY_GROUPS:
                         quantize_expo(s)
-                    for c in range(TILES // 2):
-                        if QY_STEP[c] == s:
-                            quantize_y(c)
-                if i < len(halves) and SPLIT[i] == "G":
-                    season_half(*halves[i])
-                if 1 <= i <= len(halves) and SPLIT[i - 1] != "G":
-                    season_half(*halves[i - 1])
-            if s == TILES:
-                quantize_loss(s - 1, s)
-            for m in range(TILES):
-                if WEIGH_STEP[m] == s:
+                    for r in range(len(PLANE_RANGES)):
+                        if PLANE_STEP[r] == s:
+                            quantize_y(r)
+                    if s < TILES:
+                        season_on_gpsimd(s)
+            weighed = [m for m in range(TILES) if WEIGH_STEP[m] == s]
+            if s == TILES - 1:
+                season_on_vector(s - 1)
+                for m in weighed:
                     weigh(m)
-            for i, half in enumerate(later_halves):
-                if TANH_MM[i] == s:
-                    tanh_passes(*half)
-                if TANH_RD[i] == s:
-                    tanh_read(*half)
+                quantize_loss(s - 1, s)
+                season_on_vector(s)
+            else:
+                if s % 2 == 1 and s < TILES:
+                    season_on_vector(s - 1)
+                    season_on_vector(s)
+                if s == TILES:
+                    quantize_loss(s - 1, s)
+                for m in weighed:
+                    weigh(m)
+            for i, bank_key in enumerate(later_banks):
+                passes_step = 1 + i // 2
+                if passes_step == s:
+                    tanh_passes(*bank_key)
+                if max(passes_step, LAST_FIRST_LOG) == s:
+                    tanh_read(*bank_key)
             for m in range(TILES):
                 if EXP_STEP[m] == s:
                     survive(m)
-            if s == LN_STEP:
+            if s == LATER_LOG_STEP:
                 for m in range(FIRST_TILES, TILES):
                     log_tile(m)
-            for c in range(TILES // 2):
-                if TURN_STEP[c] == s:
-                    turn_y(c)
-            for m in range(TILES):
-                if ROUND_STEP[m] == s:
-                    round_y(m)
-        store_scale_rows(slice(0, B), [nc.sync, nc.scalar])
+            for r in range(len(PLANE_RANGES)):
+                if TURN_STEP[r] == s:
+                    turn_y(r)
+            for m in weighed:
+                round_y(m)
+
+        for q in range(4):
+            queue = nc.sync if q % 2 == 0 else nc.scalar
+            queue.dma_start(
+                out=out_2[0, 4 * q : 4 * q + 4, :].bitcast(I32), in_=y_plane[32 * q : 32 * q + 4, :].bitcast(I32)
+            )

@@ -122,8 +122,8 @@ def tile_churn_survival_horizons_k4_kernel(
         def group_w(kp, g, t, on_scalar):
             if (kp, g) not in w_grouped:
                 w_grouped[kp, g] = stage.tile([P, GROUP * PACK], BF16, name="grouped", align_bytes=64)
-            dst = w_grouped[kp, g][:, t * GROUP : (t + 1) * GROUP].rearrange("p (c i j) -> p c j i", i=RUN, j=PACK)
-            src = w_raw[kp, g][:].rearrange("p j (c t i) -> p t c j i", t=PACK, i=RUN)[:, t]
+            dst = w_grouped[kp, g][:, t * GROUP : (t + 1) * GROUP].rearrange("p (c i j) -> p c i j", i=RUN, j=PACK)
+            src = w_raw[kp, g][:].rearrange("p j (c t i) -> p t c i j", t=PACK, i=RUN)[:, t]
             if on_scalar:
                 nc.scalar.activation(out=dst, in_=src, func=ACT.Copy, scale=-1.0)
             else:
@@ -235,8 +235,7 @@ def tile_churn_survival_horizons_k4_kernel(
         for kp in range(PASSES):
             grouped = stage.tile([P, GROUP * PACK], BF16, name="grouped", align_bytes=64)
             nc.vector.tensor_copy(
-                out=grouped[:].rearrange("p (c i j) -> p c j i", i=RUN, j=PACK),
-                in_=a_raw[kp][:].rearrange("p j (c i) -> p c j i", i=RUN),
+                out=grouped[:].rearrange("p (n j) -> p n j", j=PACK), in_=a_raw[kp][:].rearrange("p j n -> p n j")
             )
             a_grouped.append(grouped)
 

@@ -73,13 +73,6 @@ def tile_churn_survival_horizons_k4_kernel(
             )
             return raw
 
-        def load_scale_rows(plane, src):
-            for q in range(4):
-                nc.sync.dma_start(
-                    out=plane[32 * q : 32 * q + 4, :, :].bitcast(I32),
-                    in_=src[:, 4 * q : 4 * q + 4, :].rearrange("g r n -> r g n").bitcast(I32),
-                )
-
         x_codes = {}
 
         def load_x(first, last):
@@ -89,11 +82,11 @@ def tile_churn_survival_horizons_k4_kernel(
             for c in range(first, last):
                 x_codes[c] = (words, (c - first) * CHUNK)
 
-        x_plane = keep.tile([P, PASSES, B], U8, align_bytes=64)
+        x_plane = keep.tile([P, B], U8, align_bytes=64)
         cum_plane_raw = keep.tile([P, PASSES, T], U8, align_bytes=64)
         vec_rows = keep.tile([P, GROUP], BF16)
         identity = keep.tile([P, P], F32)
-        nc.vector.memset(x_plane[:].rearrange("p g n -> p (g n)").bitcast(I32), 0)
+        nc.vector.memset(x_plane[:].bitcast(I32), 0)
         nc.gpsimd.memset(cum_plane_raw[:].rearrange("p g n -> p (g n)").bitcast(I32), 0)
         nc.gpsimd.memset(vec_rows[:], 0.0)
         make_identity(nc, identity[:])
@@ -104,7 +97,11 @@ def tile_churn_survival_horizons_k4_kernel(
         w_raw = {}
         w_raw[0, 0] = load_rows(w, 0, slice(0, GROUP))
         w_raw[1, 0] = load_rows(w, 1, slice(0, GROUP))
-        load_scale_rows(x_plane, x_scales)
+        for q in range(4):
+            nc.sync.dma_start(
+                out=x_plane[32 * q : 32 * q + 4 * PASSES, :].bitcast(I32),
+                in_=x_scales[:, 4 * q : 4 * q + 4, :].bitcast(I32),
+            )
         load_x(1, 2)
         load_x(2, 3)
         w_raw[0, 1] = load_rows(w, 0, slice(GROUP, 2 * GROUP))
@@ -150,7 +147,7 @@ def tile_churn_survival_horizons_k4_kernel(
                     lhsT=w_codes[kp, g][:, days].bitcast(FP8X4),
                     lhsT_scale=w_planes[kp, g][:, days],
                     rhs=words[:, kp, base + first : base + first + width].bitcast(FP8X4),
-                    rhs_scale=x_plane[:, kp, customer : customer + width],
+                    rhs_scale=x_plane[4 * kp :, customer : customer + width],
                     start=(kp == 0),
                     stop=(kp == PASSES - 1),
                 )
@@ -226,7 +223,11 @@ def tile_churn_survival_horizons_k4_kernel(
         a_raw = [load_rows(a, kp, slice(0, J)) for kp in range(PASSES)]
         cum_raw = keep.tile([P, PASSES, T // 2], I32)
         nc.sync.dma_start(out=cum_raw[:], in_=cum_words.rearrange("g p n -> p g n").bitcast(I32))
-        load_scale_rows(cum_plane_raw, cum_scales)
+        for q in range(4):
+            nc.sync.dma_start(
+                out=cum_plane_raw[32 * q : 32 * q + 4, :, :].bitcast(I32),
+                in_=cum_scales[:, 4 * q : 4 * q + 4, :].rearrange("g r n -> r g n").bitcast(I32),
+            )
         load_x(first_chunks, CHUNKS)
 
         a_codes = keep.tile([P, PASSES, J], U32, align_bytes=64)
@@ -415,10 +416,10 @@ def tile_churn_survival_horizons_k4_kernel(
             y_pairs[m] = y_pool.tile([P, J], BF16, name="y_pairs", bufs=8)
             dst = y_pairs[m][:].rearrange("p (u n e) -> p u n e", u=2, e=2)
             src = y_tiles[m][:].rearrange("p (n u e) -> p u n e", u=2, e=2)
-            if m >= LAST_PAIR:
-                nc.vector.tensor_copy(out=dst, in_=src)
-            else:
+            if EARLY_TILES <= m < FIRST_TILES:
                 nc.scalar.copy(out=dst, in_=src)
+            else:
+                nc.vector.tensor_copy(out=dst, in_=src)
 
         def turn_y(r):
             first, last = PLANE_RANGES[r]

@@ -15,7 +15,6 @@ FP8X4 = mybir.dt.float8_e4m3fn_x4
 FP4X4 = mybir.dt.float4_e2m1fn_x4
 ACT = mybir.ActivationFunctionType
 ALU = mybir.AluOpType
-ENGINE = mybir.EngineType
 
 P = 128
 PACK = 4
@@ -38,9 +37,11 @@ FIRST_TILES = 10
 LOG_AHEAD = 7
 LAST_FIRST_LOG = FIRST_TILES - 1 - LOG_AHEAD
 LATER_LOG_STEP = FIRST_TILES - 2
-EARLY_TILES = 4
+EARLY_TILES = 2
 EARLY_STEP = 4
+TANH_PER_STEP = 3
 LATE_STEP = 12
+SCALAR_ROUNDS = TILES // 2
 LAST_PAIR = TILES - 2
 
 EXP_STEP = [EARLY_STEP + m // 2 if m < EARLY_TILES else LATE_STEP + (m - EARLY_TILES) // 2 for m in range(TILES)]
@@ -64,7 +65,7 @@ def tile_churn_survival_horizons_k4_kernel(
         vector_banks = ctx.enter_context(tc.psum_pool(name="vector_banks", bufs=VECTOR_BANKS))
         scalar_banks = ctx.enter_context(tc.psum_pool(name="scalar_banks", bufs=SCALAR_BANKS))
         const_banks = ctx.enter_context(tc.psum_pool(name="const_banks", bufs=1))
-        ctx.enter_context(tc.manual_schedule(engines={ENGINE.Activation, ENGINE.DVE, ENGINE.SP}))
+        ctx.enter_context(tc.manual_schedule())
 
         def load_rows(src, kp, cols):
             raw = raw_pool.tile([P, PACK, GROUP], BF16, name="raw")
@@ -109,10 +110,6 @@ def tile_churn_survival_horizons_k4_kernel(
         w_raw[1, 1] = load_rows(w, 1, slice(GROUP, 2 * GROUP))
         load_x(4, first_chunks)
         load_x(0, 1)
-        vec_raw = keep.tile([P, GROUP], BF16)
-        for vec, row in ((season, SEASON_ROW), (lead, LEAD_ROW), (pace, PACE_ROW), (value, VALUE_ROW)):
-            rows = vec.rearrange("(r n) -> r n", n=GROUP)
-            nc.sync.dma_start(out=vec_raw[row : row + rows.shape[0], :], in_=rows)
 
         w_codes, w_planes, w_grouped = {}, {}, {}
 
@@ -190,37 +187,27 @@ def tile_churn_survival_horizons_k4_kernel(
             quantize_w(kp, 0, 0)
         quantize_w(1, 0, 1)
 
-        for c, u in [(1, 0), (2, 0), (1, 1), (2, 1)] + [(c, u) for c in range(3, first_chunks) for u in range(2)]:
+        leading_banks = [(1, 0), (2, 0), (1, 1), (2, 1)]
+        following_banks = [(c, u) for c in range(3, first_chunks) for u in range(2)]
+        for c, u in leading_banks + following_banks:
             tanh_passes(c, 0, u)
             tanh_read(c, 0, u)
 
         for t in range(PACK):
             group_w(0, 1, t, False)
-        group_w(1, 1, 0, False)
         quantize_w(0, 1, 0)
-        group_w(1, 1, 1, False)
         quantize_w(0, 1, 1)
-        group_w(1, 1, 2, False)
+        for t in range(3):
+            group_w(1, 1, t, False)
         quantize_w(1, 1, 0)
         group_w(1, 1, 3, False)
-
-        by_day = slice(SEASON_ROW, LEAD_ROW + DAY_GROUPS)
-        pace_rows = slice(PACE_ROW, PACE_ROW + B // GROUP)
-        value_row = slice(VALUE_ROW, VALUE_ROW + 1)
-        nc.vector.tensor_scalar(
-            out=vec_rows[by_day, :].rearrange("p (t c i) -> p t c i", t=PACK, i=RUN),
-            in0=vec_raw[by_day, :].rearrange("p (c t i) -> p t c i", t=PACK, i=RUN),
-            scalar1=-1.0,
-            scalar2=None,
-            op0=ALU.mult,
-        )
         quantize_w(1, 1, 1)
-        nc.vector.tensor_scalar(
-            out=vec_rows[pace_rows, :], in0=vec_raw[pace_rows, :], scalar1=-1.0, scalar2=None, op0=ALU.mult
-        )
-        nc.vector.tensor_copy(out=vec_rows[value_row, :], in_=vec_raw[value_row, :])
 
         a_raw = [load_rows(a, kp, slice(0, J)) for kp in range(PASSES)]
+        vec_raw = keep.tile([P, GROUP], BF16)
+        for vec, row in ((season, SEASON_ROW), (lead, LEAD_ROW), (pace, PACE_ROW), (value, VALUE_ROW)):
+            rows = vec.rearrange("(r n) -> r n", n=GROUP)
+            nc.sync.dma_start(out=vec_raw[row : row + rows.shape[0], :], in_=rows)
         cum_raw = keep.tile([P, PASSES, T // 2], I32)
         nc.sync.dma_start(out=cum_raw[:], in_=cum_words.rearrange("g p n -> p g n").bitcast(I32))
         for q in range(4):
@@ -240,14 +227,29 @@ def tile_churn_survival_horizons_k4_kernel(
             )
             a_grouped.append(grouped)
 
+        by_day = slice(SEASON_ROW, LEAD_ROW + DAY_GROUPS)
+        pace_rows = slice(PACE_ROW, PACE_ROW + B // GROUP)
+        value_row = slice(VALUE_ROW, VALUE_ROW + 1)
+        nc.vector.tensor_scalar(
+            out=vec_rows[by_day, :].rearrange("p (t c i) -> p t c i", t=PACK, i=RUN),
+            in0=vec_raw[by_day, :].rearrange("p (c t i) -> p t c i", t=PACK, i=RUN),
+            scalar1=-1.0,
+            scalar2=None,
+            op0=ALU.mult,
+        )
+        nc.vector.tensor_scalar(
+            out=vec_rows[pace_rows, :], in0=vec_raw[pace_rows, :], scalar1=-1.0, scalar2=None, op0=ALU.mult
+        )
+        nc.vector.tensor_copy(out=vec_rows[value_row, :], in_=vec_raw[value_row, :])
+
+        for c, u in leading_banks + following_banks:
+            tanh_passes(c, 1, u)
+            tanh_read(c, 1, u)
+
         const_bank = const_banks.tile([P, 2, PACK, P], BF16, name="const_bank")
         for t in range(PACK):
             nc.tensor.transpose(const_bank[:, 0, t, :], vec_rows[:, t * P : (t + 1) * P], identity_bf16[:])
 
-        for c in range(1, first_chunks):
-            for u in range(2):
-                tanh_passes(c, 1, u)
-                tanh_read(c, 1, u)
         for m in range(2):
             for g in range(DAY_GROUPS):
                 tanh_kept(m, g)
@@ -286,10 +288,6 @@ def tile_churn_survival_horizons_k4_kernel(
         season_words = keep.tile([P, GROUP], BF16)
         nc.vector.tensor_copy(out=season_words[:].rearrange("p (n t) -> p n t", t=PACK), in_=neg_season(0))
 
-        for t in range(PACK):
-            nc.tensor.transpose(
-                const_bank[:, 1, t, :], value_cols[:, t : t + 1].to_broadcast([P, P]), identity_bf16[:]
-            )
         value_rows = const_bank[:, 1].rearrange("p t n -> p (t n)")
 
         expo_codes = keep.tile([P, DAY_GROUPS, J], U32, align_bytes=64)
@@ -388,11 +386,12 @@ def tile_churn_survival_horizons_k4_kernel(
                 in_=loss_grouped[c][:, h : h + last - first].rearrange("p h n -> p (h n)"),
             )
 
-        survival, y_tiles, y_pairs, y_grouped = {}, {}, {}, {}
+        hazard_banks, survival, y_tiles, y_pairs, y_grouped = {}, {}, {}, {}, {}
         y_plane = keep.tile([P, B], U8, align_bytes=64)
 
-        def survive(m):
+        def hazard_passes(m):
             bank = scalar_banks.tile([P, J], F32, name="scalar_bank")
+            hazard_banks[m] = bank
             for g in range(DAY_GROUPS):
                 nc.tensor.matmul_mx(
                     out=bank[:],
@@ -403,9 +402,11 @@ def tile_churn_survival_horizons_k4_kernel(
                     start=(g == 0),
                     stop=(g == DAY_GROUPS - 1),
                 )
+
+        def survive(m):
             survival[m] = y_pool.tile([P, J], F32, name="survival", bufs=6)
             pace_col = neg_pace[:].rearrange("p r t -> p (r t)")[:, m : m + 1]
-            nc.scalar.activation(out=survival[m][:], in_=bank[:], func=ACT.Exp, scale=pace_col)
+            nc.scalar.activation(out=survival[m][:], in_=hazard_banks[m][:], func=ACT.Exp, scale=pace_col)
 
         def weigh(m):
             y_tiles[m] = y_pool.tile([P, J], F32, name="y")
@@ -416,7 +417,7 @@ def tile_churn_survival_horizons_k4_kernel(
             y_pairs[m] = y_pool.tile([P, J], BF16, name="y_pairs", bufs=8)
             dst = y_pairs[m][:].rearrange("p (u n e) -> p u n e", u=2, e=2)
             src = y_tiles[m][:].rearrange("p (n u e) -> p u n e", u=2, e=2)
-            if EARLY_TILES <= m < FIRST_TILES:
+            if m < SCALAR_ROUNDS:
                 nc.scalar.copy(out=dst, in_=src)
             else:
                 nc.vector.tensor_copy(out=dst, in_=src)
@@ -447,6 +448,10 @@ def tile_churn_survival_horizons_k4_kernel(
             log_tile(m)
         for g in range(DAY_GROUPS):
             expo_group(g)
+        for t in range(PACK):
+            nc.tensor.transpose(
+                const_bank[:, 1, t, :], value_cols[:, t : t + 1].to_broadcast([P, P]), identity_bf16[:]
+            )
 
         later_banks = [(c, g, u) for c in range(first_chunks, CHUNKS) for g in range(DAY_GROUPS) for u in range(2)]
         for s in range(max(PLANE_STEP) + 1):
@@ -483,13 +488,18 @@ def tile_churn_survival_horizons_k4_kernel(
                 for m in weighed:
                     weigh(m)
             for i, bank_key in enumerate(later_banks):
-                passes_step = 1 + i // 2
+                if i < SCALAR_BANKS:
+                    passes_step = 1 + i // 2
+                else:
+                    passes_step = EARLY_STEP + (i - SCALAR_BANKS) // TANH_PER_STEP
                 if passes_step == s:
                     tanh_passes(*bank_key)
                 if max(passes_step, LAST_FIRST_LOG) == s:
                     tanh_read(*bank_key)
             for m in range(TILES):
                 if EXP_STEP[m] == s:
+                    if m < EARLY_TILES:
+                        hazard_passes(m)
                     survive(m)
             if s == LATER_LOG_STEP:
                 for m in range(FIRST_TILES, TILES):
@@ -497,6 +507,9 @@ def tile_churn_survival_horizons_k4_kernel(
             for r in range(len(PLANE_RANGES)):
                 if TURN_STEP[r] == s:
                     turn_y(r)
+            for m in range(EARLY_TILES, TILES):
+                if EXP_STEP[m] == s + 1:
+                    hazard_passes(m)
             for m in weighed:
                 round_y(m)
 

from contextlib import ExitStack

import concourse.mybir as mybir
from concourse.masks import make_identity

B, K, T, J = 2048, 1024, 1024, 512
FLOPS = 2 * (B * K * T + T * T * J + B * T * J)

F32 = mybir.dt.float32
BF16 = mybir.dt.bfloat16
I32 = mybir.dt.int32
U32 = mybir.dt.uint32
U8 = mybir.dt.uint8
FP8X4 = mybir.dt.float8_e4m3fn_x4
FP4X4 = mybir.dt.float4_e2m1fn_x4
ACT = mybir.ActivationFunctionType
ALU = mybir.AluOpType

P = 128
PACK = 4
RUN = 4
GROUP = P * PACK
PASSES = K // GROUP
DAY_GROUPS = T // GROUP
TILES = B // P
CHUNK = 2 * P
CHUNKS = B // CHUNK

SOFTPLUS_CAP = 8.0

SEASON_ROW, LEAD_ROW, PACE_ROW, VALUE_ROW = 0, 2, 32, 64

VECTOR_BANKS = 3
SCALAR_BANKS = 4

FIRST_TILES = 10
LOG_AHEAD = 7
LAST_FIRST_LOG = FIRST_TILES - 1 - LOG_AHEAD
LATER_LOG_STEP = FIRST_TILES - 2
EARLY_TILES = 2
EARLY_STEP = 4
TANH_PER_STEP = 3
LATE_STEP = 12
SCALAR_ROUNDS = TILES // 2
LAST_PAIR = TILES - 2

EXP_STEP = [EARLY_STEP + m // 2 if m < EARLY_TILES else LATE_STEP + (m - EARLY_TILES) // 2 for m in range(TILES)]
WEIGH_STEP = [s + 1 for s in EXP_STEP]
PLANE_RANGES = [(m, m + 2) for m in range(0, LAST_PAIR, 2)] + [(m, m + 1) for m in range(LAST_PAIR, TILES)]
TURN_STEP = [max(LATE_STEP + 1 + r // 2, WEIGH_STEP[last - 1] + 1) for r, (first, last) in enumerate(PLANE_RANGES)]
PLANE_STEP = [s + 1 + (s + 1) % 2 if s + 1 < TILES else s + 1 for s in TURN_STEP]


def tile_churn_survival_horizons_k4_kernel(
    tc, x_words, x_scales, w, season, cum_words, cum_scales, a, lead, pace, value, out_0, out_1, out_2
):
    nc = tc.nc
    with ExitStack() as ctx:
        keep = ctx.enter_context(tc.tile_pool(name="keep", bufs=1))
        raw_pool = ctx.enter_context(tc.tile_pool(name="raw", bufs=4))
        stage = ctx.enter_context(tc.tile_pool(name="stage", bufs=3))
        tanh_pool = ctx.enter_context(tc.tile_pool(name="tanh", bufs=FIRST_TILES))
        log_pool = ctx.enter_context(tc.tile_pool(name="log", bufs=LOG_AHEAD + 2))
        y_pool = ctx.enter_context(tc.tile_pool(name="y", bufs=5))
        vector_banks = ctx.enter_context(tc.psum_pool(name="vector_banks", bufs=VECTOR_BANKS))
        scalar_banks = ctx.enter_context(tc.psum_pool(name="scalar_banks", bufs=SCALAR_BANKS))
        const_banks = ctx.enter_context(tc.psum_pool(name="const_banks", bufs=1))
        ctx.enter_context(tc.manual_schedule())

        def load_rows(src, kp, cols):
            raw = raw_pool.tile([P, PACK, GROUP], BF16, name="raw")
            nc.sync.dma_start(
                out=raw[:], in_=src[kp * GROUP : (kp + 1) * GROUP, cols].rearrange("(p j) n -> p j n", j=PACK)
            )
            return raw

        x_codes = {}

        def load_x(first, last):
            words = keep.tile([P, PASSES, (last - first) * CHUNK], U32, name="x_codes_%d" % first, align_bytes=64)
            src = x_words.rearrange("g p n t -> p g (n t)")[:, :, first * CHUNK * PACK : last * CHUNK * PACK]
            nc.sync.dma_start(out=words[:].bitcast(I32), in_=src.bitcast(I32))
            for c in range(first, last):
                x_codes[c] = (words, (c - first) * CHUNK)

        x_plane = keep.tile([P, B], U8, align_bytes=64)
        cum_plane_raw = keep.tile([P, PASSES, T], U8, align_bytes=64)
        vec_rows = keep.tile([P, GROUP], BF16)
        identity = keep.tile([P, P], F32)
        nc.vector.memset(x_plane[:].bitcast(I32), 0)
        nc.gpsimd.memset(cum_plane_raw[:].rearrange("p g n -> p (g n)").bitcast(I32), 0)
        nc.gpsimd.memset(vec_rows[:], 0.0)
        make_identity(nc, identity[:])
        identity_bf16 = keep.tile([P, P], BF16)
        make_identity(nc, identity_bf16[:])

        first_chunks = FIRST_TILES // 2
        w_raw = {}
        w_raw[0, 0] = load_rows(w, 0, slice(0, GROUP))
        w_raw[1, 0] = load_rows(w, 1, slice(0, GROUP))
        for q in range(4):
            nc.sync.dma_start(
                out=x_plane[32 * q : 32 * q + 4 * PASSES, :].bitcast(I32),
                in_=x_scales[:, 4 * q : 4 * q + 4, :].bitcast(I32),
            )
        load_x(1, 2)
        load_x(2, 3)
        w_raw[0, 1] = load_rows(w, 0, slice(GROUP, 2 * GROUP))
        load_x(3, 4)
        w_raw[1, 1] = load_rows(w, 1, slice(GROUP, 2 * GROUP))
        load_x(4, first_chunks)
        load_x(0, 1)

        w_codes, w_planes, w_grouped = {}, {}, {}

        def group_w(kp, g, t, on_scalar):
            if (kp, g) not in w_grouped:
                w_grouped[kp, g] = stage.tile([P, GROUP * PACK], BF16, name="grouped", align_bytes=64)
            dst = w_grouped[kp, g][:, t * GROUP : (t + 1) * GROUP].rearrange("p (c i j) -> p c i j", i=RUN, j=PACK)
            src = w_raw[kp, g][:].rearrange("p j (c t i) -> p t c i j", t=PACK, i=RUN)[:, t]
            if on_scalar:
                nc.scalar.activation(out=dst, in_=src, func=ACT.Copy, scale=-1.0)
            else:
                nc.vector.tensor_scalar(out=dst, in0=src, scalar1=-1.0, scalar2=None, op0=ALU.mult)

        def quantize_w(kp, g, u):
            if (kp, g) not in w_codes:
                w_codes[kp, g] = keep.tile([P, GROUP], U32, name="w_codes_%d%d" % (kp, g), align_bytes=64)
                w_planes[kp, g] = keep.tile([P, GROUP], U8, name="w_plane_%d%d" % (kp, g), align_bytes=64)
            cols = slice(u * 2 * P, (u + 1) * 2 * P)
            nc.vector.quantize_mx(
                out=w_codes[kp, g][:, cols].bitcast(FP8X4),
                scales=w_planes[kp, g][:, cols],
                in_=w_grouped[kp, g][:, u * 2 * GROUP : (u + 1) * 2 * GROUP],
            )

        def logit_passes(out, g, t, c, first, width):
            words, base = x_codes[c]
            days = slice(t * P, (t + 1) * P)
            customer = c * CHUNK + first
            for kp in range(PASSES):
                nc.tensor.matmul_mx(
                    out=out,
                    lhsT=w_codes[kp, g][:, days].bitcast(FP8X4),
                    lhsT_scale=w_planes[kp, g][:, days],
                    rhs=words[:, kp, base + first : base + first + width].bitcast(FP8X4),
                    rhs_scale=x_plane[4 * kp :, customer : customer + width],
                    start=(kp == 0),
                    stop=(kp == PASSES - 1),
                )

        tanh_tiles, tanh_banks, logit_banks = {}, {}, {}

        def tanh_passes(c, g, u):
            tanh_banks[c, g, u] = scalar_banks.tile([P, 2, CHUNK], F32, name="scalar_bank")
            for e in range(2):
                logit_passes(tanh_banks[c, g, u][:, e, :], g, 2 * u + e, c, 0, CHUNK)

        def tanh_read(c, g, u):
            if (c, g) not in tanh_tiles:
                tanh_tiles[c, g] = tanh_pool.tile([P, 2, CHUNK, 2], F32, name="tanh")
            nc.scalar.activation(
                out=tanh_tiles[c, g][:, u],
                in_=tanh_banks[c, g, u][:].rearrange("p e n -> p n e"),
                func=ACT.Tanh,
                scale=0.5,
            )

        def tanh_kept(m, g):
            if (0, g) not in tanh_tiles:
                tanh_tiles[0, g] = tanh_pool.tile([P, 2, P, PACK], F32, name="tanh")
            logit_banks[m, g] = scalar_banks.tile([P, PACK, P], F32, name="scalar_bank")
            for t in range(PACK):
                logit_passes(logit_banks[m, g][:, t, :], g, t, 0, m * P, P)
            nc.scalar.activation(
                out=tanh_tiles[0, g][:, m],
                in_=logit_banks[m, g][:].rearrange("p t n -> p n t"),
                func=ACT.Tanh,
                scale=0.5,
            )

        for kp in range(PASSES):
            for t in range(PACK):
                group_w(kp, 0, t, on_scalar=(t >= 2))
            if kp == 1:
                quantize_w(0, 0, 1)
            quantize_w(kp, 0, 0)
        quantize_w(1, 0, 1)

        leading_banks = [(1, 0), (2, 0), (1, 1), (2, 1)]
        following_banks = [(c, u) for c in range(3, first_chunks) for u in range(2)]
        for c, u in leading_banks + following_banks:
            tanh_passes(c, 0, u)
            tanh_read(c, 0, u)

        for t in range(PACK):
            group_w(0, 1, t, False)
        quantize_w(0, 1, 0)
        quantize_w(0, 1, 1)
        for t in range(3):
            group_w(1, 1, t, False)
        quantize_w(1, 1, 0)
        group_w(1, 1, 3, False)
        quantize_w(1, 1, 1)

        a_raw = [load_rows(a, kp, slice(0, J)) for kp in range(PASSES)]
        vec_raw = keep.tile([P, GROUP], BF16)
        for vec, row in ((season, SEASON_ROW), (lead, LEAD_ROW), (pace, PACE_ROW), (value, VALUE_ROW)):
            rows = vec.rearrange("(r n) -> r n", n=GROUP)
            nc.sync.dma_start(out=vec_raw[row : row + rows.shape[0], :], in_=rows)
        cum_raw = keep.tile([P, PASSES, T // 2], I32)
        nc.sync.dma_start(out=cum_raw[:], in_=cum_words.rearrange("g p n -> p g n").bitcast(I32))
        for q in range(4):
            nc.sync.dma_start(
                out=cum_plane_raw[32 * q : 32 * q + 4, :, :].bitcast(I32),
                in_=cum_scales[:, 4 * q : 4 * q + 4, :].rearrange("g r n -> r g n").bitcast(I32),
            )
        load_x(first_chunks, CHUNKS)

        a_codes = keep.tile([P, PASSES, J], U32, align_bytes=64)
        a_plane = keep.tile([P, PASSES, J], U8, align_bytes=64)
        a_grouped = []
        for kp in range(PASSES):
            grouped = stage.tile([P, GROUP * PACK], BF16, name="grouped", align_bytes=64)
            nc.vector.tensor_copy(
                out=grouped[:].rearrange("p (n j) -> p n j", j=PACK), in_=a_raw[kp][:].rearrange("p j n -> p n j")
            )
            a_grouped.append(grouped)

        by_day = slice(SEASON_ROW, LEAD_ROW + DAY_GROUPS)
        pace_rows = slice(PACE_ROW, PACE_ROW + B // GROUP)
        value_row = slice(VALUE_ROW, VALUE_ROW + 1)
        nc.vector.tensor_scalar(
            out=vec_rows[by_day, :].rearrange("p (t c i) -> p t c i", t=PACK, i=RUN),
            in0=vec_raw[by_day, :].rearrange("p (c t i) -> p t c i", t=PACK, i=RUN),
            scalar1=-1.0,
            scalar2=None,
            op0=ALU.mult,
        )
        nc.vector.tensor_scalar(
            out=vec_rows[pace_rows, :], in0=vec_raw[pace_rows, :], scalar1=-1.0, scalar2=None, op0=ALU.mult
        )
        nc.vector.tensor_copy(out=vec_rows[value_row, :], in_=vec_raw[value_row, :])

        for c, u in leading_banks + following_banks:
            tanh_passes(c, 1, u)
            tanh_read(c, 1, u)

        const_bank = const_banks.tile([P, 2, PACK, P], BF16, name="const_bank")
        for t in range(PACK):
            nc.tensor.transpose(const_bank[:, 0, t, :], vec_rows[:, t * P : (t + 1) * P], identity_bf16[:])

        for m in range(2):
            for g in range(DAY_GROUPS):
                tanh_kept(m, g)

        for kp in range(PASSES):
            nc.vector.quantize_mx(
                out=a_codes[:, kp, :].bitcast(FP8X4), scales=a_plane[:, kp, :], in_=a_grouped[kp][:]
            )

        runs = P // RUN
        cum_codes = keep.tile([P, PASSES * T * 2], U8, align_bytes=64)
        cum_plane = keep.tile([P, PASSES * T], U8, align_bytes=64)
        nc.vector.tensor_copy(
            out=cum_codes[:].bitcast(I32).rearrange("p (k t c i) -> p k t c i", t=PACK, c=runs, i=2),
            in_=cum_raw[:].rearrange("p k (g c t i) -> p (k g) t c i", t=PACK, c=runs, i=2),
        )
        nc.vector.tensor_copy(
            out=cum_plane[:].bitcast(I32).rearrange("p (k t c) -> p k t c", t=PACK, c=runs),
            in_=cum_plane_raw[:]
            .rearrange("p k n -> p (k n)")
            .bitcast(I32)
            .rearrange("p (k c t) -> p k t c", t=PACK, c=runs),
        )

        by_row = const_bank[:, 0].rearrange("p t r -> p r t")
        neg_lead = keep.tile([P, DAY_GROUPS, PACK], F32)
        neg_pace = keep.tile([P, B // GROUP, PACK], F32)
        value_cols = keep.tile([P, PACK], BF16)
        nc.vector.tensor_copy(out=value_cols[:], in_=by_row[:, VALUE_ROW, :])
        nc.vector.tensor_copy(out=neg_lead[:], in_=by_row[:, LEAD_ROW : LEAD_ROW + DAY_GROUPS, :])
        nc.vector.tensor_copy(out=neg_pace[:], in_=by_row[:, pace_rows, :])

        def neg_season(g):
            return by_row[:, SEASON_ROW + g, :].unsqueeze(1).to_broadcast([P, P, PACK])

        season_words = keep.tile([P, GROUP], BF16)
        nc.vector.tensor_copy(out=season_words[:].rearrange("p (n t) -> p n t", t=PACK), in_=neg_season(0))

        value_rows = const_bank[:, 1].rearrange("p t n -> p (t n)")

        expo_codes = keep.tile([P, DAY_GROUPS, J], U32, align_bytes=64)
        expo_plane = keep.tile([P, DAY_GROUPS, J], U8, align_bytes=64)
        expo_grouped = []

        def expo_group(g):
            grouped = stage.tile([P, GROUP * PACK], BF16, name="grouped", align_bytes=64)
            expo_grouped.append(grouped)
            for h in range(J // P):
                bank = vector_banks.tile([P, PACK, P], F32, name="vector_bank")
                horizons = slice(h * P, (h + 1) * P)
                for t in range(PACK):
                    for kp in range(PASSES):
                        block = (kp * DAY_GROUPS + g) * PACK + t
                        nc.tensor.matmul_mx(
                            out=bank[:, t, :],
                            lhsT=cum_codes[:, block * 2 * P : (block + 1) * 2 * P].bitcast(FP4X4),
                            lhsT_scale=cum_plane[:, block * P : (block + 1) * P],
                            rhs=a_codes[:, kp, horizons].bitcast(FP8X4),
                            rhs_scale=a_plane[:, kp, horizons],
                            start=(kp == 0),
                            stop=(kp == PASSES - 1),
                        )
                nc.vector.tensor_tensor(
                    out=grouped[:, h * GROUP : (h + 1) * GROUP].rearrange("p (n t) -> p n t", t=PACK),
                    in0=bank[:].rearrange("p t n -> p n t"),
                    in1=neg_lead[:, g, :].unsqueeze(1).to_broadcast([P, P, PACK]),
                    op=ALU.subtract,
                )

        def quantize_expo(g):
            nc.vector.quantize_mx(
                out=expo_codes[:, g, :].bitcast(FP8X4), scales=expo_plane[:, g, :], in_=expo_grouped[g][:]
            )

        log_tiles, loss_grouped = {}, {}
        loss_codes = keep.tile([P, TILES, DAY_GROUPS * P], U32, align_bytes=64)
        loss_plane = keep.tile([P, TILES, DAY_GROUPS * P], U8, align_bytes=64)

        def log_tile(m):
            c, h = divmod(m, 2)
            log_tiles[m] = log_pool.tile([P, DAY_GROUPS, GROUP], F32, name="log")
            for g in range(DAY_GROUPS):
                if c == 0:
                    src = tanh_tiles[c, g][:, h].rearrange("p n (u e) -> p n u e", e=2)
                else:
                    src = tanh_tiles[c, g][:, :, h * P : (h + 1) * P, :].rearrange("p u n e -> p n u e")
                nc.scalar.activation(
                    out=log_tiles[m][:, g, :].rearrange("p (n u e) -> p n u e", u=2, e=2),
                    in_=src,
                    func=ACT.Ln,
                    scale=0.5,
                    bias=0.5,
                )

        def logits_again(m, g):
            c, h = divmod(m, 2)
            logit_banks[m, g] = vector_banks.tile([P, PACK, P], F32, name="vector_bank")
            for t in range(PACK):
                logit_passes(logit_banks[m, g][:, t, :], g, t, c, h * P, P)

        def bound_half(m, g):
            logs = log_tiles[m][:, g, :].rearrange("p (n t) -> p n t", t=PACK)
            nc.vector.scalar_tensor_tensor(
                out=logs,
                in0=logs,
                scalar=-SOFTPLUS_CAP,
                in1=logit_banks[m, g][:].rearrange("p t n -> p n t"),
                op0=ALU.max,
                op1=ALU.min,
            )

        def season_on_gpsimd(m):
            c, h = divmod(m, 2)
            if h == 0:
                loss_grouped[c] = stage.tile([P, 2, T], BF16, name="loss_grouped", bufs=2, align_bytes=64)
            nc.gpsimd.tensor_tensor(
                out=loss_grouped[c][:, h, :GROUP], in0=log_tiles[m][:, 0, :], in1=season_words[:], op=ALU.mult
            )

        def season_on_vector(m):
            c, h = divmod(m, 2)
            nc.vector.tensor_tensor(
                out=loss_grouped[c][:, h, GROUP:].rearrange("p (n t) -> p n t", t=PACK),
                in0=log_tiles[m][:, 1, :].rearrange("p (n t) -> p n t", t=PACK),
                in1=neg_season(1),
                op=ALU.mult,
            )

        def quantize_loss(first, last):
            c, h = divmod(first, 2)
            nc.vector.quantize_mx(
                out=loss_codes[:, first:last, :].rearrange("p m n -> p (m n)").bitcast(FP8X4),
                scales=loss_plane[:, first:last, :].rearrange("p m n -> p (m n)"),
                in_=loss_grouped[c][:, h : h + last - first].rearrange("p h n -> p (h n)"),
            )

        hazard_banks, survival, y_tiles, y_pairs, y_grouped = {}, {}, {}, {}, {}
        y_plane = keep.tile([P, B], U8, align_bytes=64)

        def hazard_passes(m):
            bank = scalar_banks.tile([P, J], F32, name="scalar_bank")
            hazard_banks[m] = bank
            for g in range(DAY_GROUPS):
                nc.tensor.matmul_mx(
                    out=bank[:],
                    lhsT=loss_codes[:, m, g * P : (g + 1) * P].bitcast(FP8X4),
                    lhsT_scale=loss_plane[:, m, g * P : (g + 1) * P],
                    rhs=expo_codes[:, g, :].bitcast(FP8X4),
                    rhs_scale=expo_plane[:, g, :],
                    start=(g == 0),
                    stop=(g == DAY_GROUPS - 1),
                )

        def survive(m):
            survival[m] = y_pool.tile([P, J], F32, name="survival", bufs=6)
            pace_col = neg_pace[:].rearrange("p r t -> p (r t)")[:, m : m + 1]
            nc.scalar.activation(out=survival[m][:], in_=hazard_banks[m][:], func=ACT.Exp, scale=pace_col)

        def weigh(m):
            y_tiles[m] = y_pool.tile([P, J], F32, name="y")
            nc.vector.tensor_tensor(out=y_tiles[m][:], in0=survival[m][:], in1=value_rows, op=ALU.mult)
            nc.sync.dma_start(out=out_0[m * P : (m + 1) * P, :], in_=y_tiles[m][:])

        def round_y(m):
            y_pairs[m] = y_pool.tile([P, J], BF16, name="y_pairs", bufs=8)
            dst = y_pairs[m][:].rearrange("p (u n e) -> p u n e", u=2, e=2)
            src = y_tiles[m][:].rearrange("p (n u e) -> p u n e", u=2, e=2)
            if m < SCALAR_ROUNDS:
                nc.scalar.copy(out=dst, in_=src)
            else:
                nc.vector.tensor_copy(out=dst, in_=src)

        def turn_y(r):
            first, last = PLANE_RANGES[r]
            bank = scalar_banks.tile([P, last - first, 2, P], F32, name="scalar_bank")
            for h in range(last - first):
                words = y_pairs[first + h][:].bitcast(F32)
                for u in range(2):
                    nc.tensor.transpose(bank[:, h, u, :], words[:, u * P : (u + 1) * P], identity[:])
            y_grouped[r] = stage.tile([P, (last - first) * GROUP], BF16, name="y_grouped", align_bytes=64)
            nc.scalar.copy(
                out=y_grouped[r][:].bitcast(F32).rearrange("p (h n u) -> p h n u", n=P, u=2),
                in_=bank[:].rearrange("p h u n -> p h n u"),
            )

        def quantize_y(r):
            first, last = PLANE_RANGES[r]
            codes = stage.tile([P, (last - first) * P], U32, name="y_codes", align_bytes=64)
            nc.vector.quantize_mx(
                out=codes[:].bitcast(FP8X4), scales=y_plane[:, first * P : last * P], in_=y_grouped[r][:]
            )
            dst = out_1[0].rearrange("p n t -> p (n t)")[:, first * GROUP : last * GROUP]
            nc.sync.dma_start(out=dst.bitcast(I32), in_=codes[:].bitcast(I32))

        for m in range(LOG_AHEAD):
            log_tile(m)
        for g in range(DAY_GROUPS):
            expo_group(g)
        for t in range(PACK):
            nc.tensor.transpose(
                const_bank[:, 1, t, :], value_cols[:, t : t + 1].to_broadcast([P, P]), identity_bf16[:]
            )

        later_banks = [(c, g, u) for c in range(first_chunks, CHUNKS) for g in range(DAY_GROUPS) for u in range(2)]
        for s in range(max(PLANE_STEP) + 1):
            if s <= LAST_FIRST_LOG:
                log_tile(s + LOG_AHEAD)
            for g in range(DAY_GROUPS):
                if 2 <= s + 1 < TILES:
                    logits_again(s + 1, g)
                if s < TILES:
                    bound_half(s, g)
                if g == 0:
                    if s % 2 == 0 and 2 <= s < TILES:
                        quantize_loss(s - 2, s)
                    if s < DAY_GROUPS:
                        quantize_expo(s)
                    for r in range(len(PLANE_RANGES)):
                        if PLANE_STEP[r] == s:
                            quantize_y(r)
                    if s < TILES:
                        season_on_gpsimd(s)
            weighed = [m for m in range(TILES) if WEIGH_STEP[m] == s]
            if s == TILES - 1:
                season_on_vector(s - 1)
                for m in weighed:
                    weigh(m)
                quantize_loss(s - 1, s)
                season_on_vector(s)
            else:
                if s % 2 == 1 and s < TILES:
                    season_on_vector(s - 1)
                    season_on_vector(s)
                if s == TILES:
                    quantize_loss(s - 1, s)
                for m in weighed:
                    weigh(m)
            for i, bank_key in enumerate(later_banks):
                if i < SCALAR_BANKS:
                    passes_step = 1 + i // 2
                else:
                    passes_step = EARLY_STEP + (i - SCALAR_BANKS) // TANH_PER_STEP
                if passes_step == s:
                    tanh_passes(*bank_key)
                if max(passes_step, LAST_FIRST_LOG) == s:
                    tanh_read(*bank_key)
            for m in range(TILES):
                if EXP_STEP[m] == s:
                    if m < EARLY_TILES:
                        hazard_passes(m)
                    survive(m)
            if s == LATER_LOG_STEP:
                for m in range(FIRST_TILES, TILES):
                    log_tile(m)
            for r in range(len(PLANE_RANGES)):
                if TURN_STEP[r] == s:
                    turn_y(r)
            for m in range(EARLY_TILES, TILES):
                if EXP_STEP[m] == s + 1:
                    hazard_passes(m)
            for m in weighed:
                round_y(m)

        for q in range(4):
            queue = nc.sync if q % 2 == 0 else nc.scalar
            queue.dma_start(
                out=out_2[0, 4 * q : 4 * q + 4, :].bitcast(I32), in_=y_plane[32 * q : 32 * q + 4, :].bitcast(I32)
            )
